import numpy as np
import ml_dtypes


def mxq(x, axis, fmt="e4m3"):
    dtype, down = {"e4m3": (ml_dtypes.float8_e4m3fn, 7), "e5m2": (ml_dtypes.float8_e5m2, 14)}[fmt]
    v = np.moveaxis(np.asarray(x, np.float32).astype(ml_dtypes.bfloat16).astype(np.float64), axis, -1)
    blocks = v.reshape(v.shape[:-1] + (-1, 32))
    amax = np.abs(blocks).max(-1, keepdims=True)
    byte = np.maximum(np.where(amax > 0, np.frexp(amax)[1] - 1 + 127, 0) - down, 1)
    scale = np.exp2(byte - 127.0)
    codes = (blocks / scale).astype(np.float32).astype(dtype).astype(np.float64)
    return np.moveaxis((codes * scale).reshape(v.shape), -1, axis)


WIDE = False


def mx_kscale(k):
    if not WIDE:
        return np.ones(k)
    levels = np.array([10, -10, 5, -5, 0])
    if k % 512:
        return np.exp2(np.random.permutation(np.resize(levels, k // 32))).repeat(32)
    a = np.empty((k // 512, 16))
    for p in range(k // 512):
        a[p, :8] = np.random.permutation(np.resize(levels, 8))
        for g in range(8):
            far = levels[np.abs(levels - a[p, g]) >= 10]
            a[p, g + 8] = far[np.random.randint(len(far))]
    return np.exp2(a.ravel()).repeat(32)


BF16 = ml_dtypes.bfloat16


def bf(x):
    return np.asarray(x, np.float32).astype(BF16)


def f64(x):
    return np.asarray(x).astype(np.float64)


B, D, F, O = 1024, 512, 1024, 512


def draw0():
    s, t = mx_kscale(D), mx_kscale(F)
    return {
        "xb": bf(np.random.standard_normal((B, D)) * 0.8 * s),
        "xg": bf(np.random.standard_normal((B, D)) * s),
        "w1": bf(np.random.standard_normal((D, F)) * 0.25 / np.sqrt(D) / s[:, None]),
        "b1": bf(np.random.standard_normal(F) * 0.8),
        "gain": bf((1.0 + 0.1 * np.random.standard_normal(F)) * t),
        "w2": bf(np.random.standard_normal((F, O)) * 2.0 / np.sqrt(F) / t[:, None]),
    }


def split_bias(ub, ug, b1):
    share = (np.abs(ub) + 0.01) / (np.abs(ub) + np.abs(ug) + 0.02)
    pb = ub + share * b1
    pg = ug + (1.0 - share) * b1
    return pb, pg


def split_tanh(pb, pg):
    full = np.tanh(pb + pg)
    hb = 0.5 * (np.tanh(pb) + full - np.tanh(pg))
    hg = full - hb
    return hb, hg


def core(xb, xg, w1, b1, gain, w2):
    w1q = mxq(f64(w1), 0, "e4m3")
    ub = mxq(f64(xb), 1, "e4m3") @ w1q
    ug = mxq(f64(xg), 1, "e4m3") @ w1q
    pb, pg = split_bias(ub, ug, f64(b1))
    hb, hg = split_tanh(pb, pg)
    w2q = mxq(f64(w2), 0, "e4m3")
    g = f64(gain)
    yb = mxq(hb * g, 1, "e4m3") @ w2q
    yg = mxq(hg * g, 1, "e4m3") @ w2q
    return yb, yg


def e4m3fn_bytes(y):
    return np.clip(np.asarray(y, np.float64), -448.0, 448.0).astype(np.float32).astype(ml_dtypes.float8_e4m3fn).view(np.uint8)


def e4m3fn_values(b):
    return np.asarray(b, np.uint8).view(ml_dtypes.float8_e4m3fn).astype(np.float64)


def setup_inputs():
    d = draw0()
    x0 = np.asarray(d['xg']).astype(np.float64)
    s = (np.max(np.abs(x0), axis=(0,), keepdims=True) / 448.0).astype(np.float32)
    out = {}
    for k, v in d.items():
        if k == 'xg':
            out['xg_bytes'] = e4m3fn_bytes(x0 / s.astype(np.float64))
            out['xg_scale'] = s
        else:
            out[k] = v
    return out


def reference(xb, xg_bytes, xg_scale, w1, b1, gain, w2):
    return core(xb, e4m3fn_values(xg_bytes) * xg_scale.astype(np.float64), w1, b1, gain, w2)

@@ -1,0 +1,333 @@
+from contextlib import ExitStack
+
+import concourse.mybir as mybir
+from concourse.masks import make_identity
+
+B, D, F, O = 1024, 512, 1024, 512
+FLOPS = 2 * (2 * B * D * F + 2 * B * F * O)
+
+F32 = mybir.dt.float32
+BF16 = mybir.dt.bfloat16
+U32 = mybir.dt.uint32
+U8 = mybir.dt.uint8
+FP8 = mybir.dt.float8_e4m3fn
+FP8X4 = mybir.dt.float8_e4m3fn_x4
+ALU = mybir.AluOpType
+ACT = mybir.ActivationFunctionType
+
+P = 128
+HALF = 512
+CHUNK = 256
+NJ = F // P
+
+
+def tile_contextualdecompositiontanhlayerpair_kernel(tc, xb, xg_bytes, xg_scale, w1, b1, gain, w2, out_0, out_1):
+    nc = tc.nc
+    with ExitStack() as ctx:
+        keep = ctx.enter_context(tc.tile_pool(name="keep", bufs=1))
+        work = ctx.enter_context(tc.tile_pool(name="work", bufs=3))
+        psum = ctx.enter_context(tc.psum_pool(name="psum", bufs=1))
+        ctx.enter_context(tc.manual_schedule())
+
+        def kept(shape, dtype, name):
+            return keep.tile(shape, dtype, name=name, align_bytes=64)
+
+        def staged(shape, dtype, name):
+            return work.tile(shape, dtype, name=name, tag="staged", bufs=14, align_bytes=64)
+
+        def mx_pair(width, name):
+            return kept([P, width], U32, name + "_codes"), kept([P, width], U8, name + "_scales")
+
+        def quantize(pair, values):
+            nc.vector.quantize_mx(out=pair[0][:].bitcast(FP8X4), scales=pair[1][:], in_=values)
+
+        def mx_pass(out, left, lcols, right, rcols, start, stop):
+            nc.tensor.matmul_mx(
+                out=out,
+                lhsT=left[0][:, lcols].bitcast(FP8X4), lhsT_scale=left[1][:, lcols],
+                rhs=right[0][:, rcols].bitcast(FP8X4), rhs_scale=right[1][:, rcols],
+                start=start, stop=stop,
+            )
+
+        scale_cols = kept([P, 4], F32, "scale_cols")
+        b1_raw = kept([P, 2, 4], BF16, "b1_raw")
+        gain_raw = kept([P, 2, 4], BF16, "gain_raw")
+        nc.scalar.dma_start(out=scale_cols[:], in_=xg_scale.rearrange("o (p t) -> p (o t)", t=4))
+
+        xb_raw = [staged([P, 4 * D], BF16, "xb_raw%d" % h) for h in range(2)]
+        xg_raw = [kept([P, 4 * D], U8, "xg_bytes_raw%d" % h) for h in range(2)]
+        w1_raw = [staged([P, 4, 512], BF16, "w1_raw%d" % g) for g in range(2)]
+        x_grouped = [[staged([P, 4 * HALF], BF16, "x_grouped%d_%d" % (w, h)) for h in range(2)] for w in range(2)]
+        w1_grouped = [staged([P, 4 * 512], BF16, "w1_grouped%d" % g) for g in range(2)]
+        w2_raw = [staged([P, 4, O], BF16, "w2_raw%d" % g) for g in range(2)]
+        w2_grouped = [staged([P, 4 * O], BF16, "w2_grouped%d" % g) for g in range(2)]
+        xb_rows = xb.rearrange("(h p r) k -> h p (r k)", h=2, r=4)
+        xg_rows = xg_bytes.rearrange("(h p r) k -> h p (r k)", h=2, r=4)
+        w1_rows = w1.rearrange("(p j) (g c) -> g p j c", j=4, g=2)
+        w2_rows = w2.rearrange("(g p j) o -> g p j o", g=2, j=4)
+        nc.sync.dma_start(out=w1_raw[0][:], in_=w1_rows[0])
+        nc.sync.dma_start(out=xg_raw[0][:], in_=xg_rows[0])
+        nc.sync.dma_start(out=xb_raw[0][:], in_=xb_rows[0])
+        nc.sync.dma_start(out=xg_raw[1][:], in_=xg_rows[1])
+        nc.sync.dma_start(out=xb_raw[1][:], in_=xb_rows[1])
+        nc.sync.dma_start(out=w1_raw[1][:], in_=w1_rows[1])
+        nc.sync.dma_start(out=b1_raw[:], in_=b1.rearrange("(g p t) -> p g t", g=2, t=4))
+        nc.sync.dma_start(out=gain_raw[:], in_=gain.rearrange("(g p t) -> p g t", g=2, t=4))
+        nc.sync.dma_start(out=w2_raw[0][:], in_=w2_rows[0])
+        nc.sync.dma_start(out=w2_raw[1][:], in_=w2_rows[1])
+
+        ident = kept([P, P], F32, "ident")
+        make_identity(nc, ident[:])
+        bias = b1_raw[:].rearrange("p g t -> p (g t)")
+        neg_bias = kept([P, NJ], F32, "neg_bias")
+        half_gain = kept([P, NJ], F32, "half_gain")
+
+        def scaled_columns():
+            for dst, src, factor in ((neg_bias, b1_raw, -1.0), (half_gain, gain_raw, 0.5)):
+                nc.vector.tensor_scalar(out=dst[:], in0=src[:].rearrange("p g t -> p (g t)"), scalar1=factor, scalar2=None, op0=ALU.mult)
+
+        def in_bank(index, shape, name):
+            return psum.tile(shape, F32, name=name, tag="bank%d" % (index % 8))
+
+        scale_row = in_bank(6, [P, D], "scale_row")
+        for t in range(4):
+            nc.tensor.transpose(scale_row[:, t:D:4], scale_cols[:, t : t + 1].to_broadcast([P, P]), ident[:])
+
+        xg_wide = [[kept([P, D], BF16, "xg_wide%d_%d" % (h, r)) for r in range(4)] for h in range(2)]
+        xq = [[mx_pair(HALF, "xq%d_%d" % (w, h)) for h in range(2)] for w in range(2)]
+        w1q = [mx_pair(512, "w1q%d" % g) for g in range(2)]
+        w2q = [mx_pair(O, "w2q%d" % g) for g in range(2)]
+
+        def widen(h, r):
+            nc.vector.tensor_tensor(out=xg_wide[h][r][:], in0=xg_raw[h][:, r * D : (r + 1) * D].bitcast(FP8), in1=scale_row[:], op=ALU.mult)
+
+        def turn(w, h, rp, index):
+            bank = in_bank(index, [P, 2, 2, P], "turned")
+            for rr in range(2):
+                r = 2 * rp + rr
+                rows = xb_raw[h][:, r * D : (r + 1) * D] if w == 0 else xg_wide[h][r][:]
+                words = rows.bitcast(F32)
+                for u in range(2):
+                    nc.tensor.transpose(bank[:, rr, u, :], words[:, u : D // 2 : 2], ident[:])
+            dst = x_grouped[w][h][:].bitcast(F32)[:, rp * 512 : (rp + 1) * 512]
+            nc.scalar.copy(out=dst.rearrange("p (r n u) -> p r n u", r=2, u=2), in_=bank[:].rearrange("p r u n -> p r n u"))
+
+        def group_w1(g, copy):
+            copy(out=w1_grouped[g][:].rearrange("p (t m j) -> p t m j", t=4, j=4), in_=w1_raw[g][:].rearrange("p j (m t) -> p t m j", t=4))
+
+        def group_w2(g):
+            nc.vector.tensor_copy(out=w2_grouped[g][:].rearrange("p (c i j) -> p c j i", i=4, j=4), in_=w2_raw[g][:].rearrange("p j (c i) -> p c j i", i=4))
+
+        pb = [kept([P, NJ, HALF], F32, "pb%d" % h) for h in range(2)]
+        pg = [kept([P, NJ, HALF], F32, "pg%d" % h) for h in range(2)]
+        steps = 2 * NJ
+        u_banks, mags, recips, shares = {}, {}, {}, {}
+        every = slice(0, HALF)
+
+        def first_product(i, w):
+            h, j = divmod(i, NJ)
+            g, t = divmod(j, 4)
+            bank = in_bank(2 * i + w, [P, HALF], "u")
+            mx_pass(bank[:], w1q[g], slice(t * P, (t + 1) * P), xq[w][h], every, True, True)
+            u_banks[i, w] = bank
+
+        def magnitude(i, w):
+            if w == 0:
+                mags[i] = work.tile([P, 2, HALF], F32, name="mag", bufs=4)
+            nc.scalar.activation(out=mags[i][:, w, :], in_=u_banks[i, w][:], func=ACT.Abs)
+
+        def denominator(i):
+            den = work.tile([P, HALF], F32, name="den", bufs=4)
+            nc.vector.scalar_tensor_tensor(out=den[:], in0=mags[i][:, 0, :], scalar=0.02, in1=mags[i][:, 1, :], op0=ALU.add, op1=ALU.add)
+            recips[i] = den
+
+        def inverse_root(i):
+            nc.scalar.activation(out=recips[i][:], in_=recips[i][:], func=ACT.Abs_reciprocal_sqrt)
+
+        def square(i):
+            nc.scalar.activation(out=recips[i][:], in_=recips[i][:], func=ACT.Square)
+
+        def share_bias(i):
+            share = work.tile([P, HALF], F32, name="share", bufs=2)
+            nc.vector.scalar_tensor_tensor(out=share[:], in0=mags[i][:, 0, :], scalar=0.01, in1=recips[i][:], op0=ALU.add, op1=ALU.mult)
+            shares[i] = share
+
+        def add_bias(i):
+            h, j = divmod(i, NJ)
+            nc.vector.scalar_tensor_tensor(out=pb[h][:, j, :], in0=shares[i][:], scalar=bias[:, j : j + 1], in1=u_banks[i, 0][:], op0=ALU.mult, op1=ALU.add)
+            nc.vector.scalar_tensor_tensor(out=pg[h][:, j, :], in0=shares[i][:], scalar=neg_bias[:, j : j + 1], in1=u_banks[i, 1][:], op0=ALU.mult, op1=ALU.add)
+
+        def live(i):
+            return 0 <= i < steps
+
+        group_w1(0, lambda out, in_: nc.scalar.activation(out=out, in_=in_, func=ACT.Copy))
+        for r in range(4):
+            widen(0, r)
+        turn(1, 0, 0, 7)
+        turn(1, 0, 1, 4)
+        turn(0, 0, 0, 5)
+        turn(0, 0, 1, 2)
+        quantize(w1q[0], w1_grouped[0][:])
+        widen(1, 0)
+        widen(1, 1)
+        quantize(xq[1][0], x_grouped[1][0][:])
+        widen(1, 2)
+        quantize(xq[0][0], x_grouped[0][0][:])
+        widen(1, 3)
+        turn(0, 1, 0, 3)
+        turn(0, 1, 1, 7)
+        turn(1, 1, 0, 4)
+        first_product(0, 0)
+        first_product(0, 1)
+        magnitude(0, 0)
+        magnitude(0, 1)
+        turn(1, 1, 1, 5)
+        for i in range(1, 3):
+            first_product(i, 0)
+            first_product(i, 1)
+        group_w1(1, nc.vector.tensor_copy)
+        quantize(xq[0][1], x_grouped[0][1][:])
+        quantize(w1q[1], w1_grouped[1][:])
+        fillers = {
+            -1: [lambda: quantize(xq[1][1], x_grouped[1][1][:]), lambda: group_w2(0)],
+            0: [scaled_columns, lambda: quantize(w2q[0], w2_grouped[0][:])],
+        }
+
+        for k in range(-1, steps + 1):
+            if live(k - 1):
+                share_bias(k - 1)
+            if live(k + 1):
+                denominator(k + 1)
+            if live(k - 1):
+                add_bias(k - 1)
+            if k >= 0 and live(k + 3):
+                first_product(k + 3, 0)
+                first_product(k + 3, 1)
+            if live(k):
+                inverse_root(k)
+            if live(k + 2):
+                magnitude(k + 2, 0)
+            if live(k):
+                square(k)
+            if live(k + 2):
+                magnitude(k + 2, 1)
+            for filler in fillers.get(k, []):
+                filler()
+
+        units = 2 * (B // CHUNK)
+        parts, h_values, hq = {}, {}, {}
+        outs = [o.rearrange("(h p r) o -> h r p o", h=2, r=4) for o in (out_0, out_1)]
+
+        def tanh_split(u):
+            c, g = divmod(u, 2)
+            h, cc = divmod(c, 2)
+            cols = slice(cc * CHUNK, (cc + 1) * CHUNK)
+            js = slice(4 * g, 4 * g + 4)
+            part = work.tile([P, 4, 2, CHUNK], F32, name="part", bufs=3)
+            banks = []
+            for tp in range(2):
+                bank = in_bank(4 * u + tp - (2 if u >= 2 else 2 * u), [P, 2, CHUNK], "total")
+                for tt in range(2):
+                    t = 2 * tp + tt
+                    for w in range(2):
+                        mx_pass(bank[:, tt, :], w1q[g], slice(t * P, (t + 1) * P), xq[w][h], cols, w == 0, w == 1)
+                banks.append(bank)
+            nc.scalar.activation(out=pb[h][:, js, cols], in_=pb[h][:, js, cols], func=ACT.Tanh)
+            for t in range(4):
+                j = 4 * g + t
+                nc.scalar.activation(out=pg[h][:, j, cols], in_=pg[h][:, j, cols], func=ACT.Tanh, bias=bias[:, j : j + 1])
+            for t in range(4):
+                j = 4 * g + t
+                nc.scalar.activation(out=part[:, t, 1, :], in_=banks[t // 2][:, t % 2, :], func=ACT.Tanh, bias=bias[:, j : j + 1])
+            parts[u] = part
+            gain_on_scalar(u)
+
+        def difference(u):
+            c, g = divmod(u, 2)
+            h, cc = divmod(c, 2)
+            cols = slice(cc * CHUNK, (cc + 1) * CHUNK)
+            js = slice(4 * g, 4 * g + 4)
+            nc.vector.tensor_tensor(out=parts[u][:, :, 0, :], in0=pb[h][:, js, cols], in1=pg[h][:, js, cols], op=ALU.subtract)
+
+        def gain_on_scalar(u):
+            j = 4 * (u % 2)
+            full = parts[u][:, 0, 1, :]
+            nc.scalar.activation(out=full, in_=full, func=ACT.Copy, scale=half_gain[:, j : j + 1])
+
+        def apply_gain(u):
+            g = u % 2
+            for t in range(4):
+                j = 4 * g + t
+                both = parts[u][:, t, 0, :] if t == 0 else parts[u][:, t, :, :].rearrange("p s n -> p (s n)")
+                nc.vector.tensor_scalar(out=both, in0=both, scalar1=half_gain[:, j : j + 1], scalar2=None, op0=ALU.mult)
+
+        def combine(u, w, first, count):
+            cols = slice(first, first + count)
+            full = parts[u][:, :, 1, cols].rearrange("p t (c i) -> p c t i", i=4)
+            diff = parts[u][:, :, 0, cols].rearrange("p t (c i) -> p c t i", i=4)
+            values = staged([P, 4 * count], BF16, "h_values")
+            nc.vector.tensor_tensor(out=values[:].rearrange("p (c i t) -> p c t i", i=4, t=4), in0=full, in1=diff, op=ALU.add if w == 0 else ALU.subtract)
+            h_values[u, w, first] = values
+
+        def quantize_h(u, w, first, count):
+            if first == 0:
+                codes = work.tile([P, CHUNK], U32, name="h_codes", bufs=8, align_bytes=64)
+                scales = work.tile([P, CHUNK], U8, name="h_scales", bufs=8, align_bytes=64)
+                hq[u, w] = (codes, scales)
+            codes, scales = hq[u, w]
+            quantize((codes[:, first : first + count], scales[:, first : first + count]), h_values[u, w, first][:])
+
+        y_banks = {}
+
+        def second_product(c, w, rr):
+            bank = in_bank(4 * (2 * c + w) + 4 + rr, [P, O], "y")
+            for g in range(2):
+                mx_pass(bank[:], hq[2 * c + g, w], slice(rr * P, (rr + 1) * P), w2q[g], slice(0, O), g == 0, g == 1)
+            y_banks[c, w, rr] = bank
+
+        def store(c, w, rr, copy):
+            h, cc = divmod(c, 2)
+            result = staged([P, O], F32, "result")
+            copy(out=result[:], in_=y_banks[c, w, rr][:])
+            nc.sync.dma_start(out=outs[w][h, 2 * cc + rr], in_=result[:])
+
+        tanh_split(0)
+        group_w2(1)
+        quantize(w2q[1], w2_grouped[1][:])
+        tanh_split(1)
+        difference(0)
+        apply_gain(0)
+        last = units - 1
+        for u in range(last):
+            difference(u + 1)
+            for w in range(2):
+                combine(u, w, 0, CHUNK)
+            if u >= 2:
+                for rr in range(2):
+                    second_product((u - 2) // 2, u % 2, rr)
+            if u + 2 < units:
+                tanh_split(u + 2)
+            if u >= 2:
+                for rr in range(2):
+                    store((u - 2) // 2, u % 2, rr, nc.scalar.copy)
+            apply_gain(u + 1)
+            for w in range(2):
+                quantize_h(u, w, 0, CHUNK)
+        for rr in range(2):
+            second_product(last // 2 - 1, 1, rr)
+            store(last // 2 - 1, 1, rr, nc.scalar.copy)
+        combine(last, 0, 0, P)
+        combine(last, 1, 0, P)
+        combine(last, 0, P, P)
+        quantize_h(last, 0, 0, P)
+        quantize_h(last, 1, 0, P)
+        combine(last, 1, P, P)
+        for w in range(2):
+            second_product(last // 2, w, 0)
+            store(last // 2, w, 0, nc.scalar.copy)
+        quantize_h(last, 0, P, P)
+        quantize_h(last, 1, P, P)
+        second_product(last // 2, 0, 1)
+        second_product(last // 2, 1, 1)
+        store(last // 2, 0, 1, nc.scalar.copy)
+        store(last // 2, 1, 1, nc.vector.tensor_copy)

@@ -65,9 +65,9 @@ def tile_contextualdecompositiontanhlayerpair_kernel(tc, xb, xg_bytes, xg_scale,
         xg_rows = xg_bytes.rearrange("(h p r) k -> h p (r k)", h=2, r=4)
         w1_rows = w1.rearrange("(p j) (g c) -> g p j c", j=4, g=2)
         w2_rows = w2.rearrange("(g p j) o -> g p j o", g=2, j=4)
-        nc.sync.dma_start(out=w1_raw[0][:], in_=w1_rows[0])
-        nc.sync.dma_start(out=xg_raw[0][:], in_=xg_rows[0])
         nc.sync.dma_start(out=xb_raw[0][:], in_=xb_rows[0])
+        nc.sync.dma_start(out=xg_raw[0][:], in_=xg_rows[0])
+        nc.sync.dma_start(out=w1_raw[0][:], in_=w1_rows[0])
         nc.sync.dma_start(out=xg_raw[1][:], in_=xg_rows[1])
         nc.sync.dma_start(out=xb_raw[1][:], in_=xb_rows[1])
         nc.sync.dma_start(out=w1_raw[1][:], in_=w1_rows[1])
@@ -89,31 +89,49 @@ def tile_contextualdecompositiontanhlayerpair_kernel(tc, xb, xg_bytes, xg_scale,
         def in_bank(index, shape, name):
             return psum.tile(shape, F32, name=name, tag="bank%d" % (index % 8))
 
-        scale_row = in_bank(6, [P, D], "scale_row")
+        scale_row = kept([P, D], F32, "scale_row")
+        spread = in_bank(6, [P, 4, P], "spread")
         for t in range(4):
-            nc.tensor.transpose(scale_row[:, t:D:4], scale_cols[:, t : t + 1].to_broadcast([P, P]), ident[:])
+            nc.tensor.transpose(spread[:, t, :], scale_cols[:, t : t + 1].to_broadcast([P, P]), ident[:])
+        nc.scalar.copy(out=scale_row[:].rearrange("p (u q e) -> p u q e", u=2, e=2), in_=spread[:].rearrange("p (u e) q -> p u q e", u=2))
 
         xg_wide = [[kept([P, D], BF16, "xg_wide%d_%d" % (h, r)) for r in range(4)] for h in range(2)]
         xq = [[mx_pair(HALF, "xq%d_%d" % (w, h)) for h in range(2)] for w in range(2)]
         w1q = [mx_pair(512, "w1q%d" % g) for g in range(2)]
         w2q = [mx_pair(O, "w2q%d" % g) for g in range(2)]
 
+        turned = {}
+
         def widen(h, r):
-            nc.vector.tensor_tensor(out=xg_wide[h][r][:], in0=xg_raw[h][:, r * D : (r + 1) * D].bitcast(FP8), in1=scale_row[:], op=ALU.mult)
+            codes = xg_raw[h][:, r * D : (r + 1) * D].bitcast(FP8).rearrange("p (q u e) -> p u q e", u=2, e=2)
+            nc.vector.tensor_tensor(
+                out=xg_wide[h][r][:].rearrange("p (u q e) -> p u q e", u=2, e=2), in0=codes,
+                in1=scale_row[:].rearrange("p (u q e) -> p u q e", u=2, e=2), op=ALU.mult,
+            )
 
         def turn(w, h, rp, index):
             bank = in_bank(index, [P, 2, 2, P], "turned")
             for rr in range(2):
                 r = 2 * rp + rr
-                rows = xb_raw[h][:, r * D : (r + 1) * D] if w == 0 else xg_wide[h][r][:]
-                words = rows.bitcast(F32)
                 for u in range(2):
-                    nc.tensor.transpose(bank[:, rr, u, :], words[:, u : D // 2 : 2], ident[:])
-            dst = x_grouped[w][h][:].bitcast(F32)[:, rp * 512 : (rp + 1) * 512]
-            nc.scalar.copy(out=dst.rearrange("p (r n u) -> p r n u", r=2, u=2), in_=bank[:].rearrange("p r u n -> p r n u"))
+                    if w == 0:
+                        words = xb_raw[h][:, r * D : (r + 1) * D].bitcast(F32)[:, u : D // 2 : 2]
+                    else:
+                        words = xg_wide[h][r][:].bitcast(F32)[:, u * P : (u + 1) * P]
+                    nc.tensor.transpose(bank[:, rr, u, :], words, ident[:])
+            turned[w, h, rp] = bank
 
-        def group_w1(g, copy):
-            copy(out=w1_grouped[g][:].rearrange("p (t m j) -> p t m j", t=4, j=4), in_=w1_raw[g][:].rearrange("p j (m t) -> p t m j", t=4))
+        def gather(w, h, rp, copy=nc.scalar.copy):
+            bank = turned[w, h, rp]
+            dst = x_grouped[w][h][:].bitcast(F32)[:, rp * 512 : (rp + 1) * 512]
+            copy(out=dst.rearrange("p (r n u) -> p r n u", r=2, u=2), in_=bank[:].rearrange("p r u n -> p r n u"))
+
+        def group_w1(g, ts, copy):
+            copy(out=w1_grouped[g][:].rearrange("p (t m j) -> p t m j", t=4, j=4)[:, ts], in_=w1_raw[g][:].rearrange("p j (m t) -> p t m j", t=4)[:, ts])
+
+        def quantize_w1(g, ts):
+            cols = slice(ts.start * P, ts.stop * P)
+            quantize((w1q[g][0][:, cols], w1q[g][1][:, cols]), w1_grouped[g][:, 4 * cols.start : 4 * cols.stop])
 
         def group_w2(g):
             nc.vector.tensor_copy(out=w2_grouped[g][:].rearrange("p (c i j) -> p c j i", i=4, j=4), in_=w2_raw[g][:].rearrange("p j (c i) -> p c j i", i=4))
@@ -132,7 +150,7 @@ def tile_contextualdecompositiontanhlayerpair_kernel(tc, xb, xg_bytes, xg_scale,
             u_banks[i, w] = bank
 
         def magnitude(i, w):
-            if w == 0:
+            if i not in mags:
                 mags[i] = work.tile([P, 2, HALF], F32, name="mag", bufs=4)
             nc.scalar.activation(out=mags[i][:, w, :], in_=u_banks[i, w][:], func=ACT.Abs)
 
@@ -160,47 +178,65 @@ def tile_contextualdecompositiontanhlayerpair_kernel(tc, xb, xg_bytes, xg_scale,
         def live(i):
             return 0 <= i < steps
 
-        group_w1(0, lambda out, in_: nc.scalar.activation(out=out, in_=in_, func=ACT.Copy))
+        low, high, both = slice(0, 2), slice(2, 4), slice(0, 4)
         for r in range(4):
             widen(0, r)
-        turn(1, 0, 0, 7)
-        turn(1, 0, 1, 4)
-        turn(0, 0, 0, 5)
-        turn(0, 0, 1, 2)
-        quantize(w1q[0], w1_grouped[0][:])
+        turn(0, 0, 0, 7)
+        turn(0, 0, 1, 4)
+        turn(1, 0, 0, 5)
+        turn(1, 0, 1, 2)
+        gather(0, 0, 0)
+        group_w1(0, high, lambda out, in_: nc.scalar.activation(out=out, in_=in_, func=ACT.Copy))
+        gather(0, 0, 1)
+        gather(1, 0, 0)
+        gather(1, 0, 1)
+        group_w1(0, low, nc.vector.tensor_copy)
         widen(1, 0)
-        widen(1, 1)
-        quantize(xq[1][0], x_grouped[1][0][:])
-        widen(1, 2)
         quantize(xq[0][0], x_grouped[0][0][:])
-        widen(1, 3)
-        turn(0, 1, 0, 3)
-        turn(0, 1, 1, 7)
-        turn(1, 1, 0, 4)
-        first_product(0, 0)
-        first_product(0, 1)
-        magnitude(0, 0)
-        magnitude(0, 1)
-        turn(1, 1, 1, 5)
-        for i in range(1, 3):
-            first_product(i, 0)
-            first_product(i, 1)
-        group_w1(1, nc.vector.tensor_copy)
+        quantize_w1(0, both)
+        quantize(xq[1][0], x_grouped[1][0][:])
+        for r in range(1, 4):
+            widen(1, r)
+        turn(0, 1, 0, 7)
+        gather(0, 1, 0)
+        group_w1(1, high, nc.scalar.copy)
+        for i in range(2):
+            for w in range(2):
+                first_product(i, w)
+                magnitude(i, w)
+        turn(0, 1, 1, 6)
+        gather(0, 1, 1)
+        first_product(2, 0)
+        first_product(2, 1)
+        turn(1, 1, 0, 7)
+        turn(1, 1, 1, 6)
+        group_w1(1, low, nc.vector.tensor_copy)
+        denominator(0)
+        quantize_w1(1, both)
+        denominator(1)
+        gather(1, 1, 0, nc.vector.tensor_copy)
+        gather(1, 1, 1, nc.vector.tensor_copy)
+        scaled_columns()
         quantize(xq[0][1], x_grouped[0][1][:])
-        quantize(w1q[1], w1_grouped[1][:])
-        fillers = {
-            -1: [lambda: quantize(xq[1][1], x_grouped[1][1][:]), lambda: group_w2(0)],
-            0: [scaled_columns, lambda: quantize(w2q[0], w2_grouped[0][:])],
-        }
+        inverse_root(0)
+        magnitude(2, 0)
+        square(0)
+        magnitude(2, 1)
+        first_product(3, 0)
+        first_product(3, 1)
 
-        for k in range(-1, steps + 1):
-            if live(k - 1):
-                share_bias(k - 1)
+        for k in range(1, steps + 1):
+            share_bias(k - 1)
             if live(k + 1):
                 denominator(k + 1)
-            if live(k - 1):
-                add_bias(k - 1)
-            if k >= 0 and live(k + 3):
+            if k == 1:
+                quantize(xq[1][1], x_grouped[1][1][:])
+            if k == steps - 1:
+                group_w2(1)
+            if k == steps:
+                quantize(w2q[1], w2_grouped[1][:])
+            add_bias(k - 1)
+            if live(k + 3):
                 first_product(k + 3, 0)
                 first_product(k + 3, 1)
             if live(k):
@@ -211,12 +247,13 @@ def tile_contextualdecompositiontanhlayerpair_kernel(tc, xb, xg_bytes, xg_scale,
                 square(k)
             if live(k + 2):
                 magnitude(k + 2, 1)
-            for filler in fillers.get(k, []):
-                filler()
 
         units = 2 * (B // CHUNK)
         parts, h_values, hq = {}, {}, {}
         outs = [o.rearrange("(h p r) o -> h r p o", h=2, r=4) for o in (out_0, out_1)]
+
+        def scalar_share(u):
+            return 4 if u == units - 1 else min(u, 2)
 
         def tanh_split(u):
             c, g = divmod(u, 2)
@@ -240,7 +277,8 @@ def tile_contextualdecompositiontanhlayerpair_kernel(tc, xb, xg_bytes, xg_scale,
                 j = 4 * g + t
                 nc.scalar.activation(out=part[:, t, 1, :], in_=banks[t // 2][:, t % 2, :], func=ACT.Tanh, bias=bias[:, j : j + 1])
             parts[u] = part
-            gain_on_scalar(u)
+            for t in range(scalar_share(u)):
+                gain_on_scalar(u, t, 1)
 
         def difference(u):
             c, g = divmod(u, 2)
@@ -249,16 +287,16 @@ def tile_contextualdecompositiontanhlayerpair_kernel(tc, xb, xg_bytes, xg_scale,
             js = slice(4 * g, 4 * g + 4)
             nc.vector.tensor_tensor(out=parts[u][:, :, 0, :], in0=pb[h][:, js, cols], in1=pg[h][:, js, cols], op=ALU.subtract)
 
-        def gain_on_scalar(u):
-            j = 4 * (u % 2)
-            full = parts[u][:, 0, 1, :]
-            nc.scalar.activation(out=full, in_=full, func=ACT.Copy, scale=half_gain[:, j : j + 1])
+        def gain_on_scalar(u, t, s):
+            j = 4 * (u % 2) + t
+            values = parts[u][:, t, s, :]
+            nc.scalar.activation(out=values, in_=values, func=ACT.Copy, scale=half_gain[:, j : j + 1])
 
         def apply_gain(u):
             g = u % 2
             for t in range(4):
                 j = 4 * g + t
-                both = parts[u][:, t, 0, :] if t == 0 else parts[u][:, t, :, :].rearrange("p s n -> p (s n)")
+                both = parts[u][:, t, 0, :] if t < scalar_share(u) else parts[u][:, t, :, :].rearrange("p s n -> p (s n)")
                 nc.vector.tensor_scalar(out=both, in0=both, scalar1=half_gain[:, j : j + 1], scalar2=None, op0=ALU.mult)
 
         def combine(u, w, first, count):
@@ -279,11 +317,14 @@ def tile_contextualdecompositiontanhlayerpair_kernel(tc, xb, xg_bytes, xg_scale,
 
         y_banks = {}
 
+        def second_pass(c, w, rr, g, index):
+            if g == 0:
+                y_banks[c, w, rr] = in_bank(index, [P, O], "y")
+            mx_pass(y_banks[c, w, rr][:], hq[2 * c + g, w], slice(rr * P, (rr + 1) * P), w2q[g], slice(0, O), g == 0, g == 1)
+
         def second_product(c, w, rr):
-            bank = in_bank(4 * (2 * c + w) + 4 + rr, [P, O], "y")
             for g in range(2):
-                mx_pass(bank[:], hq[2 * c + g, w], slice(rr * P, (rr + 1) * P), w2q[g], slice(0, O), g == 0, g == 1)
-            y_banks[c, w, rr] = bank
+                second_pass(c, w, rr, g, 4 * (2 * c + w) + 4 + rr)
 
         def store(c, w, rr, copy):
             h, cc = divmod(c, 2)
@@ -292,42 +333,41 @@ def tile_contextualdecompositiontanhlayerpair_kernel(tc, xb, xg_bytes, xg_scale,
             nc.sync.dma_start(out=outs[w][h, 2 * cc + rr], in_=result[:])
 
         tanh_split(0)
-        group_w2(1)
-        quantize(w2q[1], w2_grouped[1][:])
         tanh_split(1)
         difference(0)
+        group_w2(0)
         apply_gain(0)
+        quantize(w2q[0], w2_grouped[0][:])
         last = units - 1
         for u in range(last):
             difference(u + 1)
+            if u + 1 == last:
+                for t in range(4):
+                    gain_on_scalar(last, t, 0)
             for w in range(2):
                 combine(u, w, 0, CHUNK)
-            if u >= 2:
-                for rr in range(2):
-                    second_product((u - 2) // 2, u % 2, rr)
             if u + 2 < units:
                 tanh_split(u + 2)
             if u >= 2:
                 for rr in range(2):
+                    second_product((u - 2) // 2, u % 2, rr)
+                for rr in range(2):
                     store((u - 2) // 2, u % 2, rr, nc.scalar.copy)
-            apply_gain(u + 1)
+            if u + 1 < last:
+                apply_gain(u + 1)
             for w in range(2):
                 quantize_h(u, w, 0, CHUNK)
         for rr in range(2):
             second_product(last // 2 - 1, 1, rr)
             store(last // 2 - 1, 1, rr, nc.scalar.copy)
-        combine(last, 0, 0, P)
-        combine(last, 1, 0, P)
-        combine(last, 0, P, P)
-        quantize_h(last, 0, 0, P)
-        quantize_h(last, 1, 0, P)
-        combine(last, 1, P, P)
         for w in range(2):
-            second_product(last // 2, w, 0)
-            store(last // 2, w, 0, nc.scalar.copy)
-        quantize_h(last, 0, P, P)
-        quantize_h(last, 1, P, P)
-        second_product(last // 2, 0, 1)
-        second_product(last // 2, 1, 1)
-        store(last // 2, 0, 1, nc.scalar.copy)
-        store(last // 2, 1, 1, nc.vector.tensor_copy)
+            for rr in range(2):
+                second_pass(last // 2, w, rr, 0, 2 + 4 * w + rr)
+        order = [(0, 0), (1, 0), (0, 1), (1, 1)]
+        combine(last, 0, 0, P)
+        for n, (w, rr) in enumerate(order):
+            if n + 1 < len(order):
+                combine(last, order[n + 1][0], order[n + 1][1] * P, P)
+            quantize_h(last, w, rr * P, P)
+            second_pass(last // 2, w, rr, 1, None)
+            store(last // 2, w, rr, nc.scalar.copy if n + 1 < len(order) else nc.vector.tensor_copy)

@@ -49,11 +49,14 @@ def tile_contextualdecompositiontanhlayerpair_kernel(tc, xb, xg_bytes, xg_scale,
                 start=start, stop=stop,
             )
 
+        warm = kept([P, 1], F32, "warm")
+        nc.vector.memset(warm[:], 1.0)
         scale_cols = kept([P, 4], F32, "scale_cols")
         b1_raw = kept([P, 2, 4], BF16, "b1_raw")
         gain_raw = kept([P, 2, 4], BF16, "gain_raw")
         nc.scalar.dma_start(out=scale_cols[:], in_=xg_scale.rearrange("o (p t) -> p (o t)", t=4))
 
+        nc.scalar.activation(out=warm[:], in_=warm[:], func=ACT.Abs_reciprocal_sqrt)
         xb_raw = [staged([P, 4 * D], BF16, "xb_raw%d" % h) for h in range(2)]
         xg_raw = [kept([P, 4 * D], U8, "xg_bytes_raw%d" % h) for h in range(2)]
         w1_raw = [staged([P, 4, 512], BF16, "w1_raw%d" % g) for g in range(2)]

@@ -33,7 +33,7 @@ def tile_contextualdecompositiontanhlayerpair_kernel(tc, xb, xg_bytes, xg_scale,
             return keep.tile(shape, dtype, name=name, align_bytes=64)
 
         def staged(shape, dtype, name):
-            return work.tile(shape, dtype, name=name, tag="staged", bufs=14, align_bytes=64)
+            return work.tile(shape, dtype, name=name, tag="staged", bufs=12, align_bytes=64)
 
         def mx_pair(width, name):
             return kept([P, width], U32, name + "_codes"), kept([P, width], U8, name + "_scales")
@@ -61,9 +61,9 @@ def tile_contextualdecompositiontanhlayerpair_kernel(tc, xb, xg_bytes, xg_scale,
         xg_raw = [kept([P, 4 * D], U8, "xg_bytes_raw%d" % h) for h in range(2)]
         w1_raw = [staged([P, 4, 512], BF16, "w1_raw%d" % g) for g in range(2)]
         x_grouped = [[staged([P, 4 * HALF], BF16, "x_grouped%d_%d" % (w, h)) for h in range(2)] for w in range(2)]
-        w1_grouped = [staged([P, 4 * 512], BF16, "w1_grouped%d" % g) for g in range(2)]
+        w1_grouped = {0: staged([P, 4 * 512], BF16, "w1_grouped")}
         w2_raw = [staged([P, 4, O], BF16, "w2_raw%d" % g) for g in range(2)]
-        w2_grouped = [staged([P, 4 * O], BF16, "w2_grouped%d" % g) for g in range(2)]
+        w2_grouped = {1: staged([P, 4 * O], BF16, "w2_grouped")}
         xb_rows = xb.rearrange("(h p r) k -> h p (r k)", h=2, r=4)
         xg_rows = xg_bytes.rearrange("(h p r) k -> h p (r k)", h=2, r=4)
         w1_rows = w1.rearrange("(p j) (g c) -> g p j c", j=4, g=2)
@@ -136,8 +136,13 @@ def tile_contextualdecompositiontanhlayerpair_kernel(tc, xb, xg_bytes, xg_scale,
             cols = slice(ts.start * P, ts.stop * P)
             quantize((w1q[g][0][:, cols], w1q[g][1][:, cols]), w1_grouped[g][:, 4 * cols.start : 4 * cols.stop])
 
-        def group_w2(g):
-            nc.vector.tensor_copy(out=w2_grouped[g][:].rearrange("p (c i j) -> p c j i", i=4, j=4), in_=w2_raw[g][:].rearrange("p j (c i) -> p c j i", i=4))
+        def group_w2(g, half):
+            cs = slice(half * O // 8, (half + 1) * O // 8)
+            nc.vector.tensor_copy(out=w2_grouped[g][:].rearrange("p (c i j) -> p c j i", i=4, j=4)[:, cs], in_=w2_raw[g][:].rearrange("p j (c i) -> p c j i", i=4)[:, cs])
+
+        def quantize_w2(g, half):
+            cols = slice(half * O // 2, (half + 1) * O // 2)
+            quantize((w2q[g][0][:, cols], w2q[g][1][:, cols]), w2_grouped[g][:, 4 * cols.start : 4 * cols.stop])
 
         pb = [kept([P, NJ, HALF], F32, "pb%d" % h) for h in range(2)]
         pg = [kept([P, NJ, HALF], F32, "pg%d" % h) for h in range(2)]
@@ -145,8 +150,13 @@ def tile_contextualdecompositiontanhlayerpair_kernel(tc, xb, xg_bytes, xg_scale,
         u_banks, mags, recips, shares = {}, {}, {}, {}
         every = slice(0, HALF)
 
+        def place(i):
+            g, rest = divmod(i, NJ)
+            h, t = divmod(rest, 4)
+            return h, 4 * g + t
+
         def first_product(i, w):
-            h, j = divmod(i, NJ)
+            h, j = place(i)
             g, t = divmod(j, 4)
             bank = in_bank(2 * i + w, [P, HALF], "u")
             mx_pass(bank[:], w1q[g], slice(t * P, (t + 1) * P), xq[w][h], every, True, True)
@@ -158,7 +168,7 @@ def tile_contextualdecompositiontanhlayerpair_kernel(tc, xb, xg_bytes, xg_scale,
             nc.scalar.activation(out=mags[i][:, w, :], in_=u_banks[i, w][:], func=ACT.Abs)
 
         def denominator(i):
-            den = work.tile([P, HALF], F32, name="den", bufs=4)
+            den = work.tile([P, HALF], F32, name="den", tag="den%d" % (i % 4), bufs=1, align_bytes=64)
             nc.vector.scalar_tensor_tensor(out=den[:], in0=mags[i][:, 0, :], scalar=0.02, in1=mags[i][:, 1, :], op0=ALU.add, op1=ALU.add)
             recips[i] = den
 
@@ -174,9 +184,24 @@ def tile_contextualdecompositiontanhlayerpair_kernel(tc, xb, xg_bytes, xg_scale,
             shares[i] = share
 
         def add_bias(i):
-            h, j = divmod(i, NJ)
+            h, j = place(i)
             nc.vector.scalar_tensor_tensor(out=pb[h][:, j, :], in0=shares[i][:], scalar=bias[:, j : j + 1], in1=u_banks[i, 0][:], op0=ALU.mult, op1=ALU.add)
             nc.vector.scalar_tensor_tensor(out=pg[h][:, j, :], in0=shares[i][:], scalar=neg_bias[:, j : j + 1], in1=u_banks[i, 1][:], op0=ALU.mult, op1=ALU.add)
+
+        pieces = {}
+        sources = [w1_raw[1][:].rearrange("p j (m t) -> p t m j", t=4)] + [w2_raw[g][:].rearrange("p j (q o) -> p q o j", q=4) for g in range(1)]
+        targets = [w1q[1], w2q[0]]
+
+        def group_piece(k):
+            n, q = divmod(k - 1, 4)
+            piece = work.tile([P, P, 4], BF16, name="piece", tag="den%d" % ((k - 1) % 4), bufs=1, align_bytes=64)
+            nc.gpsimd.tensor_scalar(out=piece[:], in0=sources[n][:, q], scalar1=1.0, scalar2=0.0, op0=ALU.mult, op1=ALU.add)
+            pieces[k] = piece
+
+        def quantize_piece(k):
+            n, q = divmod(k - 1, 4)
+            cols = slice(q * P, (q + 1) * P)
+            quantize((targets[n][0][:, cols], targets[n][1][:, cols]), pieces[k][:].rearrange("p o j -> p (o j)"))
 
         def live(i):
             return 0 <= i < steps
@@ -189,7 +214,7 @@ def tile_contextualdecompositiontanhlayerpair_kernel(tc, xb, xg_bytes, xg_scale,
         turn(1, 0, 0, 5)
         turn(1, 0, 1, 2)
         gather(0, 0, 0)
-        group_w1(0, high, lambda out, in_: nc.scalar.activation(out=out, in_=in_, func=ACT.Copy))
+        group_w1(0, high, nc.scalar.copy)
         gather(0, 0, 1)
         gather(1, 0, 0)
         gather(1, 0, 1)
@@ -201,43 +226,41 @@ def tile_contextualdecompositiontanhlayerpair_kernel(tc, xb, xg_bytes, xg_scale,
         for r in range(1, 4):
             widen(1, r)
         turn(0, 1, 0, 7)
+        turn(0, 1, 1, 6)
         gather(0, 1, 0)
-        group_w1(1, high, nc.scalar.copy)
+        gather(0, 1, 1)
         for i in range(2):
             for w in range(2):
                 first_product(i, w)
                 magnitude(i, w)
-        turn(0, 1, 1, 6)
-        gather(0, 1, 1)
-        first_product(2, 0)
-        first_product(2, 1)
         turn(1, 1, 0, 7)
         turn(1, 1, 1, 6)
-        group_w1(1, low, nc.vector.tensor_copy)
+        first_product(2, 0)
+        first_product(2, 1)
+        quantize(xq[0][1], x_grouped[0][1][:])
         denominator(0)
-        quantize_w1(1, both)
-        denominator(1)
         gather(1, 1, 0, nc.vector.tensor_copy)
+        denominator(1)
         gather(1, 1, 1, nc.vector.tensor_copy)
         scaled_columns()
-        quantize(xq[0][1], x_grouped[0][1][:])
         inverse_root(0)
         magnitude(2, 0)
         square(0)
         magnitude(2, 1)
         first_product(3, 0)
         first_product(3, 1)
+        quantize(xq[1][1], x_grouped[1][1][:])
 
         for k in range(1, steps + 1):
             share_bias(k - 1)
             if live(k + 1):
                 denominator(k + 1)
-            if k == 1:
-                quantize(xq[1][1], x_grouped[1][1][:])
-            if k == steps - 1:
-                group_w2(1)
-            if k == steps:
-                quantize(w2q[1], w2_grouped[1][:])
+            if k - 1 in pieces:
+                quantize_piece(k - 1)
+            if k <= 8:
+                group_piece(k)
+            if k >= steps - 1:
+                group_w2(1, k - steps + 1)
             add_bias(k - 1)
             if live(k + 3):
                 first_product(k + 3, 0)
@@ -338,17 +361,20 @@ def tile_contextualdecompositiontanhlayerpair_kernel(tc, xb, xg_bytes, xg_scale,
         tanh_split(0)
         tanh_split(1)
         difference(0)
-        group_w2(0)
+        quantize_w2(1, 0)
         apply_gain(0)
-        quantize(w2q[0], w2_grouped[0][:])
+        quantize_w2(1, 1)
         last = units - 1
         for u in range(last):
-            difference(u + 1)
+            if u > 0:
+                difference(u + 1)
             if u + 1 == last:
                 for t in range(4):
                     gain_on_scalar(last, t, 0)
             for w in range(2):
                 combine(u, w, 0, CHUNK)
+            if u == 0:
+                difference(1)
             if u + 2 < units:
                 tanh_split(u + 2)
             if u >= 2:
@@ -356,10 +382,12 @@ def tile_contextualdecompositiontanhlayerpair_kernel(tc, xb, xg_bytes, xg_scale,
                     second_product((u - 2) // 2, u % 2, rr)
                 for rr in range(2):
                     store((u - 2) // 2, u % 2, rr, nc.scalar.copy)
-            if u + 1 < last:
+            if 0 < u < last - 1:
                 apply_gain(u + 1)
             for w in range(2):
                 quantize_h(u, w, 0, CHUNK)
+            if u == 0:
+                apply_gain(1)
         for rr in range(2):
             second_product(last // 2 - 1, 1, rr)
             store(last // 2 - 1, 1, rr, nc.scalar.copy)

@@ -16,16 +16,25 @@ ALU = mybir.AluOpType
 ACT = mybir.ActivationFunctionType
 
 P = 128
+PACK = 4
+PASS = P * PACK
+BANKS = 8
 HALF = 512
 CHUNK = 256
-NJ = F // P
+GROUPS = F // PASS
+TILES = F // P
+STEPS = (B // HALF) * TILES
+UNITS = (B // CHUNK) * GROUPS
+XB, XG = 0, 1
+STAGED_SLOTS = 11
+SCALAR_GAIN_TILES = 2
 
 
 def tile_contextualdecompositiontanhlayerpair_kernel(tc, xb, xg_bytes, xg_scale, w1, b1, gain, w2, out_0, out_1):
     nc = tc.nc
     with ExitStack() as ctx:
         keep = ctx.enter_context(tc.tile_pool(name="keep", bufs=1))
-        work = ctx.enter_context(tc.tile_pool(name="work", bufs=3))
+        work = ctx.enter_context(tc.tile_pool(name="work", bufs=1))
         psum = ctx.enter_context(tc.psum_pool(name="psum", bufs=1))
         ctx.enter_context(tc.manual_schedule())
 
@@ -33,372 +42,364 @@ def tile_contextualdecompositiontanhlayerpair_kernel(tc, xb, xg_bytes, xg_scale,
             return keep.tile(shape, dtype, name=name, align_bytes=64)
 
         def staged(shape, dtype, name):
-            return work.tile(shape, dtype, name=name, tag="staged", bufs=12, align_bytes=64)
+            return work.tile(shape, dtype, name=name, tag="staged", bufs=STAGED_SLOTS, align_bytes=64)
 
-        def mx_pair(width, name):
+        def in_bank(index, shape, name):
+            return psum.tile(shape, F32, name=name, tag="bank%d" % (index % BANKS))
+
+        def mx_operand(width, name):
             return kept([P, width], U32, name + "_codes"), kept([P, width], U8, name + "_scales")
 
-        def quantize(pair, values):
-            nc.vector.quantize_mx(out=pair[0][:].bitcast(FP8X4), scales=pair[1][:], in_=values)
+        def quantize(operand, cols, values):
+            codes, scales = operand
+            nc.vector.quantize_mx(out=codes[:, cols].bitcast(FP8X4), scales=scales[:, cols], in_=values)
 
-        def mx_pass(out, left, lcols, right, rcols, start, stop):
+        def mx_pass(out, left, left_cols, right, right_cols, start, stop):
             nc.tensor.matmul_mx(
                 out=out,
-                lhsT=left[0][:, lcols].bitcast(FP8X4), lhsT_scale=left[1][:, lcols],
-                rhs=right[0][:, rcols].bitcast(FP8X4), rhs_scale=right[1][:, rcols],
+                lhsT=left[0][:, left_cols].bitcast(FP8X4), lhsT_scale=left[1][:, left_cols],
+                rhs=right[0][:, right_cols].bitcast(FP8X4), rhs_scale=right[1][:, right_cols],
                 start=start, stop=stop,
             )
 
+        def block(index, width=P):
+            return slice(index * width, (index + 1) * width)
+
+        whole = slice(0, PASS)
+
         warm = kept([P, 1], F32, "warm")
         nc.vector.memset(warm[:], 1.0)
-        scale_cols = kept([P, 4], F32, "scale_cols")
-        b1_raw = kept([P, 2, 4], BF16, "b1_raw")
-        gain_raw = kept([P, 2, 4], BF16, "gain_raw")
-        nc.scalar.dma_start(out=scale_cols[:], in_=xg_scale.rearrange("o (p t) -> p (o t)", t=4))
-
+        scale_cols = kept([P, PACK], F32, "scale_cols")
+        b1_raw = kept([P, GROUPS, PACK], BF16, "b1_raw")
+        gain_raw = kept([P, GROUPS, PACK], BF16, "gain_raw")
+        nc.scalar.dma_start(out=scale_cols[:], in_=xg_scale.rearrange("o (p t) -> p (o t)", t=PACK))
         nc.scalar.activation(out=warm[:], in_=warm[:], func=ACT.Abs_reciprocal_sqrt)
+
         xb_raw = [staged([P, 4 * D], BF16, "xb_raw%d" % h) for h in range(2)]
         xg_raw = [kept([P, 4 * D], U8, "xg_bytes_raw%d" % h) for h in range(2)]
-        w1_raw = [staged([P, 4, 512], BF16, "w1_raw%d" % g) for g in range(2)]
-        x_grouped = [[staged([P, 4 * HALF], BF16, "x_grouped%d_%d" % (w, h)) for h in range(2)] for w in range(2)]
-        w1_grouped = {0: staged([P, 4 * 512], BF16, "w1_grouped")}
-        w2_raw = [staged([P, 4, O], BF16, "w2_raw%d" % g) for g in range(2)]
-        w2_grouped = {1: staged([P, 4 * O], BF16, "w2_grouped")}
+        w1_raw = [staged([P, PACK, PASS], BF16, "w1_raw%d" % g) for g in range(GROUPS)]
+        x_interleaved = [[staged([P, PACK * HALF], BF16, "x_interleaved%d_%d" % (w, h)) for h in range(2)] for w in (XB, XG)]
+        w1_interleaved = staged([P, PACK * PASS], BF16, "w1_interleaved")
+        w2_raw = [staged([P, PACK, O], BF16, "w2_raw%d" % g) for g in range(GROUPS)]
         xb_rows = xb.rearrange("(h p r) k -> h p (r k)", h=2, r=4)
         xg_rows = xg_bytes.rearrange("(h p r) k -> h p (r k)", h=2, r=4)
-        w1_rows = w1.rearrange("(p j) (g c) -> g p j c", j=4, g=2)
-        w2_rows = w2.rearrange("(g p j) o -> g p j o", g=2, j=4)
+        w1_rows = w1.rearrange("(p e) (g c) -> g p e c", e=PACK, g=GROUPS)
+        w2_rows = w2.rearrange("(g p e) o -> g p e o", g=GROUPS, e=PACK)
         nc.sync.dma_start(out=xb_raw[0][:], in_=xb_rows[0])
         nc.sync.dma_start(out=xg_raw[0][:], in_=xg_rows[0])
         nc.sync.dma_start(out=w1_raw[0][:], in_=w1_rows[0])
         nc.sync.dma_start(out=xg_raw[1][:], in_=xg_rows[1])
         nc.sync.dma_start(out=xb_raw[1][:], in_=xb_rows[1])
         nc.sync.dma_start(out=w1_raw[1][:], in_=w1_rows[1])
-        nc.sync.dma_start(out=b1_raw[:], in_=b1.rearrange("(g p t) -> p g t", g=2, t=4))
-        nc.sync.dma_start(out=gain_raw[:], in_=gain.rearrange("(g p t) -> p g t", g=2, t=4))
+        nc.sync.dma_start(out=b1_raw[:], in_=b1.rearrange("(g p t) -> p g t", g=GROUPS, t=PACK))
+        nc.sync.dma_start(out=gain_raw[:], in_=gain.rearrange("(g p t) -> p g t", g=GROUPS, t=PACK))
         nc.sync.dma_start(out=w2_raw[0][:], in_=w2_rows[0])
         nc.sync.dma_start(out=w2_raw[1][:], in_=w2_rows[1])
 
         ident = kept([P, P], F32, "ident")
         make_identity(nc, ident[:])
         bias = b1_raw[:].rearrange("p g t -> p (g t)")
-        neg_bias = kept([P, NJ], F32, "neg_bias")
-        half_gain = kept([P, NJ], F32, "half_gain")
+        neg_bias = kept([P, TILES], F32, "neg_bias")
+        half_gain = kept([P, TILES], F32, "half_gain")
 
-        def scaled_columns():
+        def scale_parameters():
             for dst, src, factor in ((neg_bias, b1_raw, -1.0), (half_gain, gain_raw, 0.5)):
                 nc.vector.tensor_scalar(out=dst[:], in0=src[:].rearrange("p g t -> p (g t)"), scalar1=factor, scalar2=None, op0=ALU.mult)
 
-        def in_bank(index, shape, name):
-            return psum.tile(shape, F32, name=name, tag="bank%d" % (index % 8))
-
         scale_row = kept([P, D], F32, "scale_row")
-        spread = in_bank(6, [P, 4, P], "spread")
-        for t in range(4):
+        spread = in_bank(6, [P, PACK, P], "spread")
+        for t in range(PACK):
             nc.tensor.transpose(spread[:, t, :], scale_cols[:, t : t + 1].to_broadcast([P, P]), ident[:])
         nc.scalar.copy(out=scale_row[:].rearrange("p (u q e) -> p u q e", u=2, e=2), in_=spread[:].rearrange("p (u e) q -> p u q e", u=2))
 
         xg_wide = [[kept([P, D], BF16, "xg_wide%d_%d" % (h, r)) for r in range(4)] for h in range(2)]
-        xq = [[mx_pair(HALF, "xq%d_%d" % (w, h)) for h in range(2)] for w in range(2)]
-        w1q = [mx_pair(512, "w1q%d" % g) for g in range(2)]
-        w2q = [mx_pair(O, "w2q%d" % g) for g in range(2)]
-
+        xq = [[mx_operand(HALF, "xq%d_%d" % (w, h)) for h in range(2)] for w in (XB, XG)]
+        w1q = [mx_operand(PASS, "w1q%d" % g) for g in range(GROUPS)]
+        w2q = [mx_operand(O, "w2q%d" % g) for g in range(GROUPS)]
         turned = {}
 
         def widen(h, r):
-            codes = xg_raw[h][:, r * D : (r + 1) * D].bitcast(FP8).rearrange("p (q u e) -> p u q e", u=2, e=2)
+            codes = xg_raw[h][:, block(r, D)].bitcast(FP8).rearrange("p (q u e) -> p u q e", u=2, e=2)
             nc.vector.tensor_tensor(
                 out=xg_wide[h][r][:].rearrange("p (u q e) -> p u q e", u=2, e=2), in0=codes,
                 in1=scale_row[:].rearrange("p (u q e) -> p u q e", u=2, e=2), op=ALU.mult,
             )
 
-        def turn(w, h, rp, index):
-            bank = in_bank(index, [P, 2, 2, P], "turned")
+        def turn(w, h, pair, bank_index):
+            bank = in_bank(bank_index, [P, 2, 2, P], "turned")
             for rr in range(2):
-                r = 2 * rp + rr
+                r = 2 * pair + rr
                 for u in range(2):
-                    if w == 0:
-                        words = xb_raw[h][:, r * D : (r + 1) * D].bitcast(F32)[:, u : D // 2 : 2]
+                    if w == XB:
+                        words = xb_raw[h][:, block(r, D)].bitcast(F32)[:, u : D // 2 : 2]
                     else:
-                        words = xg_wide[h][r][:].bitcast(F32)[:, u * P : (u + 1) * P]
+                        words = xg_wide[h][r][:].bitcast(F32)[:, block(u)]
                     nc.tensor.transpose(bank[:, rr, u, :], words, ident[:])
-            turned[w, h, rp] = bank
+            turned[w, h, pair] = bank
 
-        def gather(w, h, rp, copy=nc.scalar.copy):
-            bank = turned[w, h, rp]
-            dst = x_grouped[w][h][:].bitcast(F32)[:, rp * 512 : (rp + 1) * 512]
-            copy(out=dst.rearrange("p (r n u) -> p r n u", r=2, u=2), in_=bank[:].rearrange("p r u n -> p r n u"))
+        def empty_turned(w, h, pair, copy):
+            dst = x_interleaved[w][h][:].bitcast(F32)[:, block(pair, 4 * P)]
+            copy(out=dst.rearrange("p (r n u) -> p r n u", r=2, u=2), in_=turned[w, h, pair][:].rearrange("p r u n -> p r n u"))
 
-        def group_w1(g, ts, copy):
-            copy(out=w1_grouped[g][:].rearrange("p (t m j) -> p t m j", t=4, j=4)[:, ts], in_=w1_raw[g][:].rearrange("p j (m t) -> p t m j", t=4)[:, ts])
+        def quantize_x(w, h):
+            quantize(xq[w][h], whole, x_interleaved[w][h][:])
 
-        def quantize_w1(g, ts):
-            cols = slice(ts.start * P, ts.stop * P)
-            quantize((w1q[g][0][:, cols], w1q[g][1][:, cols]), w1_grouped[g][:, 4 * cols.start : 4 * cols.stop])
+        def permuted_w1(g):
+            return w1_raw[g][:].rearrange("p e (m t) -> p t m e", t=PACK)
 
-        def group_w2(g, half):
-            cs = slice(half * O // 8, (half + 1) * O // 8)
-            nc.vector.tensor_copy(out=w2_grouped[g][:].rearrange("p (c i j) -> p c j i", i=4, j=4)[:, cs], in_=w2_raw[g][:].rearrange("p j (c i) -> p c j i", i=4)[:, cs])
+        def interleave_w1_first(tiles, copy):
+            copy(out=w1_interleaved[:].rearrange("p (t m e) -> p t m e", t=PACK, e=PACK)[:, tiles], in_=permuted_w1(0)[:, tiles])
 
-        def quantize_w2(g, half):
-            cols = slice(half * O // 2, (half + 1) * O // 2)
-            quantize((w2q[g][0][:, cols], w2q[g][1][:, cols]), w2_grouped[g][:, 4 * cols.start : 4 * cols.stop])
-
-        pb = [kept([P, NJ, HALF], F32, "pb%d" % h) for h in range(2)]
-        pg = [kept([P, NJ, HALF], F32, "pg%d" % h) for h in range(2)]
-        steps = 2 * NJ
-        u_banks, mags, recips, shares = {}, {}, {}, {}
-        every = slice(0, HALF)
+        p_parts = [[kept([P, TILES, HALF], F32, "p_part%d_%d" % (w, h)) for h in range(2)] for w in (XB, XG)]
+        u_banks, magnitudes, inverses, shares, pieces = {}, {}, {}, {}, {}
 
         def place(i):
-            g, rest = divmod(i, NJ)
-            h, t = divmod(rest, 4)
-            return h, 4 * g + t
+            g, rest = divmod(i, STEPS // GROUPS)
+            h, t = divmod(rest, PACK)
+            return h, PACK * g + t
 
         def first_product(i, w):
             h, j = place(i)
-            g, t = divmod(j, 4)
-            bank = in_bank(2 * i + w, [P, HALF], "u")
-            mx_pass(bank[:], w1q[g], slice(t * P, (t + 1) * P), xq[w][h], every, True, True)
-            u_banks[i, w] = bank
+            g, t = divmod(j, PACK)
+            u_banks[i, w] = in_bank(2 * i + w, [P, HALF], "u")
+            mx_pass(u_banks[i, w][:], w1q[g], block(t), xq[w][h], whole, True, True)
 
         def magnitude(i, w):
-            if i not in mags:
-                mags[i] = work.tile([P, 2, HALF], F32, name="mag", bufs=4)
-            nc.scalar.activation(out=mags[i][:, w, :], in_=u_banks[i, w][:], func=ACT.Abs)
+            if w == XB:
+                magnitudes[i] = work.tile([P, 2, HALF], F32, name="magnitudes", bufs=4)
+            nc.scalar.activation(out=magnitudes[i][:, w, :], in_=u_banks[i, w][:], func=ACT.Abs)
 
         def denominator(i):
-            den = work.tile([P, HALF], F32, name="den", tag="den%d" % (i % 4), bufs=1, align_bytes=64)
-            nc.vector.scalar_tensor_tensor(out=den[:], in0=mags[i][:, 0, :], scalar=0.02, in1=mags[i][:, 1, :], op0=ALU.add, op1=ALU.add)
-            recips[i] = den
+            inverses[i] = work.tile([P, HALF], F32, name="inverse", tag="inverse%d" % i, align_bytes=64)
+            nc.vector.scalar_tensor_tensor(out=inverses[i][:], in0=magnitudes[i][:, XB, :], scalar=0.02, in1=magnitudes[i][:, XG, :], op0=ALU.add, op1=ALU.add)
 
         def inverse_root(i):
-            nc.scalar.activation(out=recips[i][:], in_=recips[i][:], func=ACT.Abs_reciprocal_sqrt)
+            nc.scalar.activation(out=inverses[i][:], in_=inverses[i][:], func=ACT.Abs_reciprocal_sqrt)
 
         def square(i):
-            nc.scalar.activation(out=recips[i][:], in_=recips[i][:], func=ACT.Square)
+            nc.scalar.activation(out=inverses[i][:], in_=inverses[i][:], func=ACT.Square)
 
-        def share_bias(i):
-            share = work.tile([P, HALF], F32, name="share", bufs=2)
-            nc.vector.scalar_tensor_tensor(out=share[:], in0=mags[i][:, 0, :], scalar=0.01, in1=recips[i][:], op0=ALU.add, op1=ALU.mult)
-            shares[i] = share
+        def share(i):
+            shares[i] = work.tile([P, HALF], F32, name="share", bufs=2)
+            nc.vector.scalar_tensor_tensor(out=shares[i][:], in0=magnitudes[i][:, XB, :], scalar=0.01, in1=inverses[i][:], op0=ALU.add, op1=ALU.mult)
 
-        def add_bias(i):
+        def add_bias_share(i, w):
             h, j = place(i)
-            nc.vector.scalar_tensor_tensor(out=pb[h][:, j, :], in0=shares[i][:], scalar=bias[:, j : j + 1], in1=u_banks[i, 0][:], op0=ALU.mult, op1=ALU.add)
-            nc.vector.scalar_tensor_tensor(out=pg[h][:, j, :], in0=shares[i][:], scalar=neg_bias[:, j : j + 1], in1=u_banks[i, 1][:], op0=ALU.mult, op1=ALU.add)
+            factor = (bias, neg_bias)[w][:, j : j + 1]
+            nc.vector.scalar_tensor_tensor(out=p_parts[w][h][:, j, :], in0=shares[i][:], scalar=factor, in1=u_banks[i, w][:], op0=ALU.mult, op1=ALU.add)
 
-        pieces = {}
-        sources = [w1_raw[1][:].rearrange("p j (m t) -> p t m j", t=4)] + [w2_raw[g][:].rearrange("p j (q o) -> p q o j", q=4) for g in range(1)]
-        targets = [w1q[1], w2q[0]]
+        piece_sources = [permuted_w1(1)] + [w2_raw[g][:].rearrange("p e (q o) -> p q o e", o=P) for g in range(GROUPS)]
+        piece_targets = [w1q[1]] + w2q
+        w1_pieces = range(0, PACK)
+        w2_pieces = [range(PACK * (1 + g), PACK * (2 + g)) for g in range(GROUPS)]
 
-        def group_piece(k):
-            n, q = divmod(k - 1, 4)
-            piece = work.tile([P, P, 4], BF16, name="piece", tag="den%d" % ((k - 1) % 4), bufs=1, align_bytes=64)
-            nc.gpsimd.tensor_scalar(out=piece[:], in0=sources[n][:, q], scalar1=1.0, scalar2=0.0, op0=ALU.mult, op1=ALU.add)
-            pieces[k] = piece
+        def interleave_piece(n):
+            pieces[n] = work.tile([P, P, PACK], BF16, name="piece", tag="inverse%d" % n, align_bytes=64)
+            nc.gpsimd.tensor_scalar(out=pieces[n][:], in0=piece_sources[n // PACK][:, n % PACK], scalar1=1.0, scalar2=0.0, op0=ALU.mult, op1=ALU.add)
 
-        def quantize_piece(k):
-            n, q = divmod(k - 1, 4)
-            cols = slice(q * P, (q + 1) * P)
-            quantize((targets[n][0][:, cols], targets[n][1][:, cols]), pieces[k][:].rearrange("p o j -> p (o j)"))
+        def quantize_piece(n):
+            quantize(piece_targets[n // PACK], block(n % PACK), pieces[n][:].rearrange("p c e -> p (c e)"))
 
-        def live(i):
-            return 0 <= i < steps
-
-        low, high, both = slice(0, 2), slice(2, 4), slice(0, 4)
         for r in range(4):
             widen(0, r)
-        turn(0, 0, 0, 7)
-        turn(0, 0, 1, 4)
-        turn(1, 0, 0, 5)
-        turn(1, 0, 1, 2)
-        gather(0, 0, 0)
-        group_w1(0, high, nc.scalar.copy)
-        gather(0, 0, 1)
-        gather(1, 0, 0)
-        gather(1, 0, 1)
-        group_w1(0, low, nc.vector.tensor_copy)
+        turn(XB, 0, 0, 7)
+        turn(XB, 0, 1, 4)
+        turn(XG, 0, 0, 5)
+        turn(XG, 0, 1, 2)
+        empty_turned(XB, 0, 0, nc.scalar.copy)
+        interleave_w1_first(slice(2, 4), nc.scalar.copy)
+        empty_turned(XB, 0, 1, nc.scalar.copy)
+        empty_turned(XG, 0, 0, nc.scalar.copy)
+        empty_turned(XG, 0, 1, nc.scalar.copy)
+        interleave_w1_first(slice(0, 2), nc.vector.tensor_copy)
         widen(1, 0)
-        quantize(xq[0][0], x_grouped[0][0][:])
-        quantize_w1(0, both)
-        quantize(xq[1][0], x_grouped[1][0][:])
+        quantize_x(XB, 0)
+        quantize(w1q[0], whole, w1_interleaved[:])
+        quantize_x(XG, 0)
         for r in range(1, 4):
             widen(1, r)
-        turn(0, 1, 0, 7)
-        turn(0, 1, 1, 6)
-        gather(0, 1, 0)
-        gather(0, 1, 1)
+        turn(XB, 1, 0, 7)
+        turn(XB, 1, 1, 6)
+        empty_turned(XB, 1, 0, nc.scalar.copy)
+        empty_turned(XB, 1, 1, nc.scalar.copy)
         for i in range(2):
-            for w in range(2):
+            for w in (XB, XG):
                 first_product(i, w)
                 magnitude(i, w)
-        turn(1, 1, 0, 7)
-        turn(1, 1, 1, 6)
-        first_product(2, 0)
-        first_product(2, 1)
-        quantize(xq[0][1], x_grouped[0][1][:])
+        turn(XG, 1, 0, 7)
+        turn(XG, 1, 1, 6)
+        first_product(2, XB)
+        first_product(2, XG)
+        quantize_x(XB, 1)
         denominator(0)
-        gather(1, 1, 0, nc.vector.tensor_copy)
+        empty_turned(XG, 1, 0, nc.vector.tensor_copy)
         denominator(1)
-        gather(1, 1, 1, nc.vector.tensor_copy)
-        scaled_columns()
+        empty_turned(XG, 1, 1, nc.vector.tensor_copy)
+        scale_parameters()
         inverse_root(0)
-        magnitude(2, 0)
+        magnitude(2, XB)
         square(0)
-        magnitude(2, 1)
-        first_product(3, 0)
-        first_product(3, 1)
-        quantize(xq[1][1], x_grouped[1][1][:])
+        magnitude(2, XG)
+        first_product(3, XB)
+        first_product(3, XG)
+        quantize_x(XG, 1)
 
-        for k in range(1, steps + 1):
-            share_bias(k - 1)
-            if live(k + 1):
-                denominator(k + 1)
-            if k - 1 in pieces:
-                quantize_piece(k - 1)
-            if k <= 8:
-                group_piece(k)
-            if k >= steps - 1:
-                group_w2(1, k - steps + 1)
-            add_bias(k - 1)
-            if live(k + 3):
-                first_product(k + 3, 0)
-                first_product(k + 3, 1)
-            if live(k):
-                inverse_root(k)
-            if live(k + 2):
-                magnitude(k + 2, 0)
-            if live(k):
-                square(k)
-            if live(k + 2):
-                magnitude(k + 2, 1)
+        for i in range(1, STEPS - 1):
+            share(i - 1)
+            denominator(i + 1)
+            if i - 2 in w1_pieces:
+                quantize_piece(i - 2)
+            if i - 1 < PACK * len(piece_sources):
+                interleave_piece(i - 1)
+            add_bias_share(i - 1, XB)
+            add_bias_share(i - 1, XG)
+            if i + 3 < STEPS:
+                first_product(i + 3, XB)
+                first_product(i + 3, XG)
+            inverse_root(i)
+            if i + 2 < STEPS:
+                magnitude(i + 2, XB)
+            square(i)
+            if i + 2 < STEPS:
+                magnitude(i + 2, XG)
+        final = STEPS - 1
+        inverse_root(final)
+        share(final - 1)
+        share(final)
+        add_bias_share(final - 1, XB)
+        nc.vector.tensor_tensor(out=shares[final][:], in0=shares[final][:], in1=inverses[final][:], op=ALU.mult)
+        add_bias_share(final - 1, XG)
+        add_bias_share(final, XB)
+        add_bias_share(final, XG)
 
-        units = 2 * (B // CHUNK)
-        parts, h_values, hq = {}, {}, {}
+        DIFF, FULL = 0, 1
+        last = UNITS - 1
+        terms, h_values, hq, y_banks = {}, {}, {}, {}
         outs = [o.rearrange("(h p r) o -> h r p o", h=2, r=4) for o in (out_0, out_1)]
 
-        def scalar_share(u):
-            return 4 if u == units - 1 else min(u, 2)
+        def unit_place(u):
+            chunk, g = divmod(u, GROUPS)
+            h, chunk_in_half = divmod(chunk, HALF // CHUNK)
+            return h, block(chunk_in_half, CHUNK), g
 
-        def tanh_split(u):
-            c, g = divmod(u, 2)
-            h, cc = divmod(c, 2)
-            cols = slice(cc * CHUNK, (cc + 1) * CHUNK)
-            js = slice(4 * g, 4 * g + 4)
-            part = work.tile([P, 4, 2, CHUNK], F32, name="part", bufs=3)
-            banks = []
-            for tp in range(2):
-                bank = in_bank(4 * u + tp - (2 if u >= 2 else 2 * u), [P, 2, CHUNK], "total")
-                for tt in range(2):
-                    t = 2 * tp + tt
-                    for w in range(2):
-                        mx_pass(bank[:, tt, :], w1q[g], slice(t * P, (t + 1) * P), xq[w][h], cols, w == 0, w == 1)
-                banks.append(bank)
-            nc.scalar.activation(out=pb[h][:, js, cols], in_=pb[h][:, js, cols], func=ACT.Tanh)
-            for t in range(4):
-                j = 4 * g + t
-                nc.scalar.activation(out=pg[h][:, j, cols], in_=pg[h][:, j, cols], func=ACT.Tanh, bias=bias[:, j : j + 1])
-            for t in range(4):
-                j = 4 * g + t
-                nc.scalar.activation(out=part[:, t, 1, :], in_=banks[t // 2][:, t % 2, :], func=ACT.Tanh, bias=bias[:, j : j + 1])
-            parts[u] = part
-            for t in range(scalar_share(u)):
-                gain_on_scalar(u, t, 1)
+        def scalar_gain_tiles(u):
+            return PACK if u == last else min(u, SCALAR_GAIN_TILES)
 
-        def difference(u):
-            c, g = divmod(u, 2)
-            h, cc = divmod(c, 2)
-            cols = slice(cc * CHUNK, (cc + 1) * CHUNK)
-            js = slice(4 * g, 4 * g + 4)
-            nc.vector.tensor_tensor(out=parts[u][:, :, 0, :], in0=pb[h][:, js, cols], in1=pg[h][:, js, cols], op=ALU.subtract)
-
-        def gain_on_scalar(u, t, s):
-            j = 4 * (u % 2) + t
-            values = parts[u][:, t, s, :]
+        def gain_on_scalar(u, t, term):
+            j = PACK * (u % GROUPS) + t
+            values = terms[u][:, t, term, :]
             nc.scalar.activation(out=values, in_=values, func=ACT.Copy, scale=half_gain[:, j : j + 1])
 
-        def apply_gain(u):
-            g = u % 2
-            for t in range(4):
-                j = 4 * g + t
-                both = parts[u][:, t, 0, :] if t < scalar_share(u) else parts[u][:, t, :, :].rearrange("p s n -> p (s n)")
-                nc.vector.tensor_scalar(out=both, in0=both, scalar1=half_gain[:, j : j + 1], scalar2=None, op0=ALU.mult)
+        def tanh_split(u):
+            h, cols, g = unit_place(u)
+            terms[u] = work.tile([P, PACK, 2, CHUNK], F32, name="terms", bufs=3)
+            banks = [in_bank(4 * u + n, [P, 2, CHUNK], "total") for n in range(2)]
+            for t in range(PACK):
+                for w in (XB, XG):
+                    mx_pass(banks[t // 2][:, t % 2, :], w1q[g], block(t), xq[w][h], cols, w == XB, w == XG)
+            pb = p_parts[XB][h][:, block(g, PACK), cols]
+            nc.scalar.activation(out=pb, in_=pb, func=ACT.Tanh)
+            for t in range(PACK):
+                j = PACK * g + t
+                pg = p_parts[XG][h][:, j, cols]
+                nc.scalar.activation(out=pg, in_=pg, func=ACT.Tanh, bias=bias[:, j : j + 1])
+            for t in range(PACK):
+                j = PACK * g + t
+                nc.scalar.activation(out=terms[u][:, t, FULL, :], in_=banks[t // 2][:, t % 2, :], func=ACT.Tanh, bias=bias[:, j : j + 1])
+            for t in range(scalar_gain_tiles(u)):
+                gain_on_scalar(u, t, FULL)
 
-        def combine(u, w, first, count):
-            cols = slice(first, first + count)
-            full = parts[u][:, :, 1, cols].rearrange("p t (c i) -> p c t i", i=4)
-            diff = parts[u][:, :, 0, cols].rearrange("p t (c i) -> p c t i", i=4)
-            values = staged([P, 4 * count], BF16, "h_values")
-            nc.vector.tensor_tensor(out=values[:].rearrange("p (c i t) -> p c t i", i=4, t=4), in0=full, in1=diff, op=ALU.add if w == 0 else ALU.subtract)
-            h_values[u, w, first] = values
+        def difference(u):
+            h, cols, g = unit_place(u)
+            tiles = block(g, PACK)
+            nc.vector.tensor_tensor(out=terms[u][:, :, DIFF, :], in0=p_parts[XB][h][:, tiles, cols], in1=p_parts[XG][h][:, tiles, cols], op=ALU.subtract)
 
-        def quantize_h(u, w, first, count):
-            if first == 0:
+        def gain_on_vector(u):
+            for t in range(PACK):
+                j = PACK * (u % GROUPS) + t
+                if t < scalar_gain_tiles(u):
+                    values = terms[u][:, t, DIFF, :]
+                else:
+                    values = terms[u][:, t, :, :].rearrange("p s n -> p (s n)")
+                nc.vector.tensor_scalar(out=values, in0=values, scalar1=half_gain[:, j : j + 1], scalar2=None, op0=ALU.mult)
+
+        def combine(u, w, cols):
+            full = terms[u][:, :, FULL, cols].rearrange("p t (c i) -> p c t i", i=4)
+            diff = terms[u][:, :, DIFF, cols].rearrange("p t (c i) -> p c t i", i=4)
+            values = staged([P, PACK * (cols.stop - cols.start)], BF16, "h_values")
+            nc.vector.tensor_tensor(out=values[:].rearrange("p (c i t) -> p c t i", i=4, t=PACK), in0=full, in1=diff, op=(ALU.add, ALU.subtract)[w])
+            h_values[u, w, cols.start] = values
+
+        def quantize_h(u, w, cols):
+            if cols.start == 0:
                 codes = work.tile([P, CHUNK], U32, name="h_codes", bufs=8, align_bytes=64)
                 scales = work.tile([P, CHUNK], U8, name="h_scales", bufs=8, align_bytes=64)
                 hq[u, w] = (codes, scales)
-            codes, scales = hq[u, w]
-            quantize((codes[:, first : first + count], scales[:, first : first + count]), h_values[u, w, first][:])
+            quantize(hq[u, w], cols, h_values[u, w, cols.start][:])
 
-        y_banks = {}
+        def second_pass(chunk, w, rr, g):
+            mx_pass(y_banks[chunk, w, rr][:], hq[GROUPS * chunk + g, w], block(rr), w2q[g], whole, g == 0, g == GROUPS - 1)
 
-        def second_pass(c, w, rr, g, index):
-            if g == 0:
-                y_banks[c, w, rr] = in_bank(index, [P, O], "y")
-            mx_pass(y_banks[c, w, rr][:], hq[2 * c + g, w], slice(rr * P, (rr + 1) * P), w2q[g], slice(0, O), g == 0, g == 1)
+        def second_product(chunk, w, rr):
+            y_banks[chunk, w, rr] = in_bank(4 * w + 2 + rr, [P, O], "y")
+            for g in range(GROUPS):
+                second_pass(chunk, w, rr, g)
 
-        def second_product(c, w, rr):
-            for g in range(2):
-                second_pass(c, w, rr, g, 4 * (2 * c + w) + 4 + rr)
-
-        def store(c, w, rr, copy):
-            h, cc = divmod(c, 2)
+        def store(chunk, w, rr, copy):
+            h, chunk_in_half = divmod(chunk, HALF // CHUNK)
             result = staged([P, O], F32, "result")
-            copy(out=result[:], in_=y_banks[c, w, rr][:])
-            nc.sync.dma_start(out=outs[w][h, 2 * cc + rr], in_=result[:])
+            copy(out=result[:], in_=y_banks[chunk, w, rr][:])
+            nc.sync.dma_start(out=outs[w][h, 2 * chunk_in_half + rr], in_=result[:])
 
+        chunk_cols = slice(0, CHUNK)
         tanh_split(0)
         tanh_split(1)
         difference(0)
-        quantize_w2(1, 0)
-        apply_gain(0)
-        quantize_w2(1, 1)
-        last = units - 1
+        for n in w2_pieces[0]:
+            quantize_piece(n)
+        gain_on_vector(0)
+        for n in w2_pieces[1]:
+            quantize_piece(n)
         for u in range(last):
             if u > 0:
                 difference(u + 1)
             if u + 1 == last:
-                for t in range(4):
-                    gain_on_scalar(last, t, 0)
-            for w in range(2):
-                combine(u, w, 0, CHUNK)
+                for t in range(PACK):
+                    gain_on_scalar(last, t, DIFF)
+            for w in (XB, XG):
+                combine(u, w, chunk_cols)
             if u == 0:
                 difference(1)
-            if u + 2 < units:
+            if u + 2 < UNITS:
                 tanh_split(u + 2)
-            if u >= 2:
+            if u >= GROUPS:
+                done_chunk, w = divmod(u - GROUPS, GROUPS)
                 for rr in range(2):
-                    second_product((u - 2) // 2, u % 2, rr)
+                    second_product(done_chunk, w, rr)
                 for rr in range(2):
-                    store((u - 2) // 2, u % 2, rr, nc.scalar.copy)
+                    store(done_chunk, w, rr, nc.scalar.copy)
             if 0 < u < last - 1:
-                apply_gain(u + 1)
-            for w in range(2):
-                quantize_h(u, w, 0, CHUNK)
+                gain_on_vector(u + 1)
+            for w in (XB, XG):
+                quantize_h(u, w, chunk_cols)
             if u == 0:
-                apply_gain(1)
+                gain_on_vector(1)
+
+        last_chunk = last // GROUPS
         for rr in range(2):
-            second_product(last // 2 - 1, 1, rr)
-            store(last // 2 - 1, 1, rr, nc.scalar.copy)
-        for w in range(2):
+            second_product(last_chunk - 1, XG, rr)
+            store(last_chunk - 1, XG, rr, nc.scalar.copy)
+        for w in (XB, XG):
             for rr in range(2):
-                second_pass(last // 2, w, rr, 0, 2 + 4 * w + rr)
-        order = [(0, 0), (1, 0), (0, 1), (1, 1)]
-        combine(last, 0, 0, P)
+                y_banks[last_chunk, w, rr] = in_bank(4 * w + rr, [P, O], "y")
+                second_pass(last_chunk, w, rr, 0)
+        order = [(w, rr) for rr in range(2) for w in (XB, XG)]
+        combine(last, XB, block(0))
         for n, (w, rr) in enumerate(order):
-            if n + 1 < len(order):
-                combine(last, order[n + 1][0], order[n + 1][1] * P, P)
-            quantize_h(last, w, rr * P, P)
-            second_pass(last // 2, w, rr, 1, None)
-            store(last // 2, w, rr, nc.scalar.copy if n + 1 < len(order) else nc.vector.tensor_copy)
+            is_final = n + 1 == len(order)
+            if not is_final:
+                next_w, next_rr = order[n + 1]
+                combine(last, next_w, block(next_rr))
+            quantize_h(last, w, block(rr))
+            second_pass(last_chunk, w, rr, GROUPS - 1)
+            store(last_chunk, w, rr, nc.vector.tensor_copy if is_final else nc.scalar.copy)

from contextlib import ExitStack

import concourse.mybir as mybir
from concourse.masks import make_identity

B, D, F, O = 1024, 512, 1024, 512
FLOPS = 2 * (2 * B * D * F + 2 * B * F * O)

F32 = mybir.dt.float32
BF16 = mybir.dt.bfloat16
U32 = mybir.dt.uint32
U8 = mybir.dt.uint8
FP8 = mybir.dt.float8_e4m3fn
FP8X4 = mybir.dt.float8_e4m3fn_x4
ALU = mybir.AluOpType
ACT = mybir.ActivationFunctionType

P = 128
PACK = 4
PASS = P * PACK
BANKS = 8
HALF = 512
CHUNK = 256
GROUPS = F // PASS
TILES = F // P
STEPS = (B // HALF) * TILES
UNITS = (B // CHUNK) * GROUPS
XB, XG = 0, 1
STAGED_SLOTS = 11
SCALAR_GAIN_TILES = 2


def tile_contextualdecompositiontanhlayerpair_kernel(tc, xb, xg_bytes, xg_scale, w1, b1, gain, w2, out_0, out_1):
    nc = tc.nc
    with ExitStack() as ctx:
        keep = ctx.enter_context(tc.tile_pool(name="keep", bufs=1))
        work = ctx.enter_context(tc.tile_pool(name="work", bufs=1))
        psum = ctx.enter_context(tc.psum_pool(name="psum", bufs=1))
        ctx.enter_context(tc.manual_schedule())

        def kept(shape, dtype, name):
            return keep.tile(shape, dtype, name=name, align_bytes=64)

        def staged(shape, dtype, name):
            return work.tile(shape, dtype, name=name, tag="staged", bufs=STAGED_SLOTS, align_bytes=64)

        def in_bank(index, shape, name):
            return psum.tile(shape, F32, name=name, tag="bank%d" % (index % BANKS))

        def mx_operand(width, name):
            return kept([P, width], U32, name + "_codes"), kept([P, width], U8, name + "_scales")

        def quantize(operand, cols, values):
            codes, scales = operand
            nc.vector.quantize_mx(out=codes[:, cols].bitcast(FP8X4), scales=scales[:, cols], in_=values)

        def mx_pass(out, left, left_cols, right, right_cols, start, stop):
            nc.tensor.matmul_mx(
                out=out,
                lhsT=left[0][:, left_cols].bitcast(FP8X4), lhsT_scale=left[1][:, left_cols],
                rhs=right[0][:, right_cols].bitcast(FP8X4), rhs_scale=right[1][:, right_cols],
                start=start, stop=stop,
            )

        def block(index, width=P):
            return slice(index * width, (index + 1) * width)

        whole = slice(0, PASS)

        warm = kept([P, 1], F32, "warm")
        nc.vector.memset(warm[:], 1.0)
        scale_cols = kept([P, PACK], F32, "scale_cols")
        b1_raw = kept([P, GROUPS, PACK], BF16, "b1_raw")
        gain_raw = kept([P, GROUPS, PACK], BF16, "gain_raw")
        nc.scalar.dma_start(out=scale_cols[:], in_=xg_scale.rearrange("o (p t) -> p (o t)", t=PACK))
        nc.scalar.activation(out=warm[:], in_=warm[:], func=ACT.Abs_reciprocal_sqrt)

        xb_raw = [staged([P, 4 * D], BF16, "xb_raw%d" % h) for h in range(2)]
        xg_raw = [kept([P, 4 * D], U8, "xg_bytes_raw%d" % h) for h in range(2)]
        w1_raw = [staged([P, PACK, PASS], BF16, "w1_raw%d" % g) for g in range(GROUPS)]
        x_interleaved = [[staged([P, PACK * HALF], BF16, "x_interleaved%d_%d" % (w, h)) for h in range(2)] for w in (XB, XG)]
        w1_interleaved = staged([P, PACK * PASS], BF16, "w1_interleaved")
        w2_raw = [staged([P, PACK, O], BF16, "w2_raw%d" % g) for g in range(GROUPS)]
        xb_rows = xb.rearrange("(h p r) k -> h p (r k)", h=2, r=4)
        xg_rows = xg_bytes.rearrange("(h p r) k -> h p (r k)", h=2, r=4)
        w1_rows = w1.rearrange("(p e) (g c) -> g p e c", e=PACK, g=GROUPS)
        w2_rows = w2.rearrange("(g p e) o -> g p e o", g=GROUPS, e=PACK)
        nc.sync.dma_start(out=xb_raw[0][:], in_=xb_rows[0])
        nc.sync.dma_start(out=xg_raw[0][:], in_=xg_rows[0])
        nc.sync.dma_start(out=w1_raw[0][:], in_=w1_rows[0])
        nc.sync.dma_start(out=xg_raw[1][:], in_=xg_rows[1])
        nc.sync.dma_start(out=xb_raw[1][:], in_=xb_rows[1])
        nc.sync.dma_start(out=w1_raw[1][:], in_=w1_rows[1])
        nc.sync.dma_start(out=b1_raw[:], in_=b1.rearrange("(g p t) -> p g t", g=GROUPS, t=PACK))
        nc.sync.dma_start(out=gain_raw[:], in_=gain.rearrange("(g p t) -> p g t", g=GROUPS, t=PACK))
        nc.sync.dma_start(out=w2_raw[0][:], in_=w2_rows[0])
        nc.sync.dma_start(out=w2_raw[1][:], in_=w2_rows[1])

        ident = kept([P, P], F32, "ident")
        make_identity(nc, ident[:])
        bias = b1_raw[:].rearrange("p g t -> p (g t)")
        neg_bias = kept([P, TILES], F32, "neg_bias")
        half_gain = kept([P, TILES], F32, "half_gain")

        def scale_parameters():
            for dst, src, factor in ((neg_bias, b1_raw, -1.0), (half_gain, gain_raw, 0.5)):
                nc.vector.tensor_scalar(out=dst[:], in0=src[:].rearrange("p g t -> p (g t)"), scalar1=factor, scalar2=None, op0=ALU.mult)

        scale_row = kept([P, D], F32, "scale_row")
        spread = in_bank(6, [P, PACK, P], "spread")
        for t in range(PACK):
            nc.tensor.transpose(spread[:, t, :], scale_cols[:, t : t + 1].to_broadcast([P, P]), ident[:])
        nc.scalar.copy(out=scale_row[:].rearrange("p (u q e) -> p u q e", u=2, e=2), in_=spread[:].rearrange("p (u e) q -> p u q e", u=2))

        xg_wide = [[kept([P, D], BF16, "xg_wide%d_%d" % (h, r)) for r in range(4)] for h in range(2)]
        xq = [[mx_operand(HALF, "xq%d_%d" % (w, h)) for h in range(2)] for w in (XB, XG)]
        w1q = [mx_operand(PASS, "w1q%d" % g) for g in range(GROUPS)]
        w2q = [mx_operand(O, "w2q%d" % g) for g in range(GROUPS)]
        turned = {}

        def widen(h, r):
            codes = xg_raw[h][:, block(r, D)].bitcast(FP8).rearrange("p (q u e) -> p u q e", u=2, e=2)
            nc.vector.tensor_tensor(
                out=xg_wide[h][r][:].rearrange("p (u q e) -> p u q e", u=2, e=2), in0=codes,
                in1=scale_row[:].rearrange("p (u q e) -> p u q e", u=2, e=2), op=ALU.mult,
            )

        def turn(w, h, pair, bank_index):
            bank = in_bank(bank_index, [P, 2, 2, P], "turned")
            for rr in range(2):
                r = 2 * pair + rr
                for u in range(2):
                    if w == XB:
                        words = xb_raw[h][:, block(r, D)].bitcast(F32)[:, u : D // 2 : 2]
                    else:
                        words = xg_wide[h][r][:].bitcast(F32)[:, block(u)]
                    nc.tensor.transpose(bank[:, rr, u, :], words, ident[:])
            turned[w, h, pair] = bank

        def empty_turned(w, h, pair, copy):
            dst = x_interleaved[w][h][:].bitcast(F32)[:, block(pair, 4 * P)]
            copy(out=dst.rearrange("p (r n u) -> p r n u", r=2, u=2), in_=turned[w, h, pair][:].rearrange("p r u n -> p r n u"))

        def quantize_x(w, h):
            quantize(xq[w][h], whole, x_interleaved[w][h][:])

        def permuted_w1(g):
            return w1_raw[g][:].rearrange("p e (m t) -> p t m e", t=PACK)

        def interleave_w1_first(tiles, copy):
            copy(out=w1_interleaved[:].rearrange("p (t m e) -> p t m e", t=PACK, e=PACK)[:, tiles], in_=permuted_w1(0)[:, tiles])

        p_parts = [[kept([P, TILES, HALF], F32, "p_part%d_%d" % (w, h)) for h in range(2)] for w in (XB, XG)]
        u_banks, magnitudes, inverses, shares, pieces = {}, {}, {}, {}, {}

        def place(i):
            g, rest = divmod(i, STEPS // GROUPS)
            h, t = divmod(rest, PACK)
            return h, PACK * g + t

        def first_product(i, w):
            h, j = place(i)
            g, t = divmod(j, PACK)
            u_banks[i, w] = in_bank(2 * i + w, [P, HALF], "u")
            mx_pass(u_banks[i, w][:], w1q[g], block(t), xq[w][h], whole, True, True)

        def magnitude(i, w):
            if w == XB:
                magnitudes[i] = work.tile([P, 2, HALF], F32, name="magnitudes", bufs=4)
            nc.scalar.activation(out=magnitudes[i][:, w, :], in_=u_banks[i, w][:], func=ACT.Abs)

        def denominator(i):
            inverses[i] = work.tile([P, HALF], F32, name="inverse", tag="inverse%d" % i, align_bytes=64)
            nc.vector.scalar_tensor_tensor(out=inverses[i][:], in0=magnitudes[i][:, XB, :], scalar=0.02, in1=magnitudes[i][:, XG, :], op0=ALU.add, op1=ALU.add)

        def inverse_root(i):
            nc.scalar.activation(out=inverses[i][:], in_=inverses[i][:], func=ACT.Abs_reciprocal_sqrt)

        def square(i):
            nc.scalar.activation(out=inverses[i][:], in_=inverses[i][:], func=ACT.Square)

        def share(i):
            shares[i] = work.tile([P, HALF], F32, name="share", bufs=2)
            nc.vector.scalar_tensor_tensor(out=shares[i][:], in0=magnitudes[i][:, XB, :], scalar=0.01, in1=inverses[i][:], op0=ALU.add, op1=ALU.mult)

        def add_bias_share(i, w):
            h, j = place(i)
            factor = (bias, neg_bias)[w][:, j : j + 1]
            nc.vector.scalar_tensor_tensor(out=p_parts[w][h][:, j, :], in0=shares[i][:], scalar=factor, in1=u_banks[i, w][:], op0=ALU.mult, op1=ALU.add)

        piece_sources = [permuted_w1(1)] + [w2_raw[g][:].rearrange("p e (q o) -> p q o e", o=P) for g in range(GROUPS)]
        piece_targets = [w1q[1]] + w2q
        w1_pieces = range(0, PACK)
        w2_pieces = [range(PACK * (1 + g), PACK * (2 + g)) for g in range(GROUPS)]

        def interleave_piece(n):
            pieces[n] = work.tile([P, P, PACK], BF16, name="piece", tag="inverse%d" % n, align_bytes=64)
            nc.gpsimd.tensor_scalar(out=pieces[n][:], in0=piece_sources[n // PACK][:, n % PACK], scalar1=1.0, scalar2=0.0, op0=ALU.mult, op1=ALU.add)

        def quantize_piece(n):
            quantize(piece_targets[n // PACK], block(n % PACK), pieces[n][:].rearrange("p c e -> p (c e)"))

        for r in range(4):
            widen(0, r)
        turn(XB, 0, 0, 7)
        turn(XB, 0, 1, 4)
        turn(XG, 0, 0, 5)
        turn(XG, 0, 1, 2)
        empty_turned(XB, 0, 0, nc.scalar.copy)
        interleave_w1_first(slice(2, 4), nc.scalar.copy)
        empty_turned(XB, 0, 1, nc.scalar.copy)
        empty_turned(XG, 0, 0, nc.scalar.copy)
        empty_turned(XG, 0, 1, nc.scalar.copy)
        interleave_w1_first(slice(0, 2), nc.vector.tensor_copy)
        widen(1, 0)
        quantize_x(XB, 0)
        quantize(w1q[0], whole, w1_interleaved[:])
        quantize_x(XG, 0)
        for r in range(1, 4):
            widen(1, r)
        turn(XB, 1, 0, 7)
        turn(XB, 1, 1, 6)
        empty_turned(XB, 1, 0, nc.scalar.copy)
        empty_turned(XB, 1, 1, nc.scalar.copy)
        for i in range(2):
            for w in (XB, XG):
                first_product(i, w)
                magnitude(i, w)
        turn(XG, 1, 0, 7)
        turn(XG, 1, 1, 6)
        first_product(2, XB)
        first_product(2, XG)
        quantize_x(XB, 1)
        denominator(0)
        empty_turned(XG, 1, 0, nc.vector.tensor_copy)
        denominator(1)
        empty_turned(XG, 1, 1, nc.vector.tensor_copy)
        scale_parameters()
        inverse_root(0)
        magnitude(2, XB)
        square(0)
        magnitude(2, XG)
        first_product(3, XB)
        first_product(3, XG)
        quantize_x(XG, 1)

        for i in range(1, STEPS - 1):
            share(i - 1)
            denominator(i + 1)
            if i - 2 in w1_pieces:
                quantize_piece(i - 2)
            if i - 1 < PACK * len(piece_sources):
                interleave_piece(i - 1)
            add_bias_share(i - 1, XB)
            add_bias_share(i - 1, XG)
            if i + 3 < STEPS:
                first_product(i + 3, XB)
                first_product(i + 3, XG)
            inverse_root(i)
            if i + 2 < STEPS:
                magnitude(i + 2, XB)
            square(i)
            if i + 2 < STEPS:
                magnitude(i + 2, XG)
        final = STEPS - 1
        inverse_root(final)
        share(final - 1)
        share(final)
        add_bias_share(final - 1, XB)
        nc.vector.tensor_tensor(out=shares[final][:], in0=shares[final][:], in1=inverses[final][:], op=ALU.mult)
        add_bias_share(final - 1, XG)
        add_bias_share(final, XB)
        add_bias_share(final, XG)

        DIFF, FULL = 0, 1
        last = UNITS - 1
        terms, h_values, hq, y_banks = {}, {}, {}, {}
        outs = [o.rearrange("(h p r) o -> h r p o", h=2, r=4) for o in (out_0, out_1)]

        def unit_place(u):
            chunk, g = divmod(u, GROUPS)
            h, chunk_in_half = divmod(chunk, HALF // CHUNK)
            return h, block(chunk_in_half, CHUNK), g

        def scalar_gain_tiles(u):
            return PACK if u == last else min(u, SCALAR_GAIN_TILES)

        def gain_on_scalar(u, t, term):
            j = PACK * (u % GROUPS) + t
            values = terms[u][:, t, term, :]
            nc.scalar.activation(out=values, in_=values, func=ACT.Copy, scale=half_gain[:, j : j + 1])

        def tanh_split(u):
            h, cols, g = unit_place(u)
            terms[u] = work.tile([P, PACK, 2, CHUNK], F32, name="terms", bufs=3)
            banks = [in_bank(4 * u + n, [P, 2, CHUNK], "total") for n in range(2)]
            for t in range(PACK):
                for w in (XB, XG):
                    mx_pass(banks[t // 2][:, t % 2, :], w1q[g], block(t), xq[w][h], cols, w == XB, w == XG)
            pb = p_parts[XB][h][:, block(g, PACK), cols]
            nc.scalar.activation(out=pb, in_=pb, func=ACT.Tanh)
            for t in range(PACK):
                j = PACK * g + t
                pg = p_parts[XG][h][:, j, cols]
                nc.scalar.activation(out=pg, in_=pg, func=ACT.Tanh, bias=bias[:, j : j + 1])
            for t in range(PACK):
                j = PACK * g + t
                nc.scalar.activation(out=terms[u][:, t, FULL, :], in_=banks[t // 2][:, t % 2, :], func=ACT.Tanh, bias=bias[:, j : j + 1])
            for t in range(scalar_gain_tiles(u)):
                gain_on_scalar(u, t, FULL)

        def difference(u):
            h, cols, g = unit_place(u)
            tiles = block(g, PACK)
            nc.vector.tensor_tensor(out=terms[u][:, :, DIFF, :], in0=p_parts[XB][h][:, tiles, cols], in1=p_parts[XG][h][:, tiles, cols], op=ALU.subtract)

        def gain_on_vector(u):
            for t in range(PACK):
                j = PACK * (u % GROUPS) + t
                if t < scalar_gain_tiles(u):
                    values = terms[u][:, t, DIFF, :]
                else:
                    values = terms[u][:, t, :, :].rearrange("p s n -> p (s n)")
                nc.vector.tensor_scalar(out=values, in0=values, scalar1=half_gain[:, j : j + 1], scalar2=None, op0=ALU.mult)

        def combine(u, w, cols):
            full = terms[u][:, :, FULL, cols].rearrange("p t (c i) -> p c t i", i=4)
            diff = terms[u][:, :, DIFF, cols].rearrange("p t (c i) -> p c t i", i=4)
            values = staged([P, PACK * (cols.stop - cols.start)], BF16, "h_values")
            nc.vector.tensor_tensor(out=values[:].rearrange("p (c i t) -> p c t i", i=4, t=PACK), in0=full, in1=diff, op=(ALU.add, ALU.subtract)[w])
            h_values[u, w, cols.start] = values

        def quantize_h(u, w, cols):
            if cols.start == 0:
                codes = work.tile([P, CHUNK], U32, name="h_codes", bufs=8, align_bytes=64)
                scales = work.tile([P, CHUNK], U8, name="h_scales", bufs=8, align_bytes=64)
                hq[u, w] = (codes, scales)
            quantize(hq[u, w], cols, h_values[u, w, cols.start][:])

        def second_pass(chunk, w, rr, g):
            mx_pass(y_banks[chunk, w, rr][:], hq[GROUPS * chunk + g, w], block(rr), w2q[g], whole, g == 0, g == GROUPS - 1)

        def second_product(chunk, w, rr):
            y_banks[chunk, w, rr] = in_bank(4 * w + 2 + rr, [P, O], "y")
            for g in range(GROUPS):
                second_pass(chunk, w, rr, g)

        def store(chunk, w, rr, copy):
            h, chunk_in_half = divmod(chunk, HALF // CHUNK)
            result = staged([P, O], F32, "result")
            copy(out=result[:], in_=y_banks[chunk, w, rr][:])
            nc.sync.dma_start(out=outs[w][h, 2 * chunk_in_half + rr], in_=result[:])

        chunk_cols = slice(0, CHUNK)
        tanh_split(0)
        tanh_split(1)
        difference(0)
        for n in w2_pieces[0]:
            quantize_piece(n)
        gain_on_vector(0)
        for n in w2_pieces[1]:
            quantize_piece(n)
        for u in range(last):
            if u > 0:
                difference(u + 1)
            if u + 1 == last:
                for t in range(PACK):
                    gain_on_scalar(last, t, DIFF)
            for w in (XB, XG):
                combine(u, w, chunk_cols)
            if u == 0:
                difference(1)
            if u + 2 < UNITS:
                tanh_split(u + 2)
            if u >= GROUPS:
                done_chunk, w = divmod(u - GROUPS, GROUPS)
                for rr in range(2):
                    second_product(done_chunk, w, rr)
                for rr in range(2):
                    store(done_chunk, w, rr, nc.scalar.copy)
            if 0 < u < last - 1:
                gain_on_vector(u + 1)
            for w in (XB, XG):
                quantize_h(u, w, chunk_cols)
            if u == 0:
                gain_on_vector(1)

        last_chunk = last // GROUPS
        for rr in range(2):
            second_product(last_chunk - 1, XG, rr)
            store(last_chunk - 1, XG, rr, nc.scalar.copy)
        for w in (XB, XG):
            for rr in range(2):
                y_banks[last_chunk, w, rr] = in_bank(4 * w + rr, [P, O], "y")
                second_pass(last_chunk, w, rr, 0)
        order = [(w, rr) for rr in range(2) for w in (XB, XG)]
        combine(last, XB, block(0))
        for n, (w, rr) in enumerate(order):
            is_final = n + 1 == len(order)
            if not is_final:
                next_w, next_rr = order[n + 1]
                combine(last, next_w, block(next_rr))
            quantize_h(last, w, block(rr))
            second_pass(last_chunk, w, rr, GROUPS - 1)
            store(last_chunk, w, rr, nc.vector.tensor_copy if is_final else nc.scalar.copy)
